import numpy as np, ml_dtypes
CORES = [25,29,65,69,153,157,193,197]
N = 8
BF = ml_dtypes.bfloat16
V, M, L, P, TV, HS = 2048, 1024, 256, 8, 6, (1, 3, 8)
def pushed(ls, s, n):
    return np.take_along_axis(ls.reshape(N, 8, 16 * M), (s & 15) * M + (((s * s >> 5) + s + 77 * n) & (M - 1)), 2)
def parts(rng):
    kd = rng.permutation(np.arange(V) & 3); pool = np.argsort(kd, kind="stable").reshape(4, V >> 2)
    own = np.where(rng.random((N, 8, V)) < 0.02, rng.integers(0, 4, (N, 8, V)), kd); proto = rng.integers(0, 16, (N, 8, 16, 4))
    x = np.clip(np.take_along_axis(proto, own[:, :, None], 3) + rng.integers(-1, 2, (N, 8, 16, V)), 0, 15)
    ls = rng.integers(0, V, (N, 8, 16, M)); s = rng.integers(0, 4096, (N, 8, L))
    n = np.where(rng.random((N, 8, L)) < 0.5, rng.integers(15, 17, (N, 8, L)), rng.integers(0, 17, (N, 8, L)))
    return kd, pool, x, ls, s, n, rng.integers(10, 30, (N, 8)), rng.integers(0, 256, (N, 8, 16))
def spell(rng, ls, s, n, kd, pool, p):
    a = kd[pushed(ls, s, n)]; b = (a + rng.integers(1, 4, a.shape)) & 3; j = np.arange(1, 17)[:, None]; sh = (N, 8, 16, L)
    k = np.where(j % np.maximum(p, 1)[:, :, None] == 0, a[:, :, None], b[:, :, None])
    cut = np.maximum(2 * p, rng.integers(0, 17, p.shape))[:, :, None]
    k = np.where((p[:, :, None] == 0) | (j >= cut), rng.integers(0, 4, sh), k)
    return pool[k, rng.integers(0, V >> 2, sh)]
def two(a, b, p):
    j = np.arange(1, 17)[:, None]; q = np.where(p == 0, 99, p)[:, :, None]
    return np.where(j % q == 0, a[:, :, None], b[:, :, None])
def pack(x, ls, w, s, n, th, wt):
    w = np.where(np.arange(16)[:, None] < n[:, :, None, :], w, 0)
    return {"x": np.ascontiguousarray(x.reshape(N, 128, V)).astype(np.float32).astype(BF), "ls": np.ascontiguousarray(ls.reshape(N, 128, M)).astype(np.int32),
            "wd": np.ascontiguousarray(w.reshape(N, 128, L)).astype(np.int32), "nl": n.astype(np.int32), "sd": s.astype(np.int32),
            "th": np.ascontiguousarray(th.reshape(N, 8, 1)).astype(np.int32), "wt": np.ascontiguousarray(wt.reshape(N, 128, 1)).astype(np.int32)}
def setup_inputs(rng):
    kd, pool, x, ls, s, n, th, wt = parts(rng); p = rng.choice(np.array((0, 0) + HS), (N, 8, L))
    return pack(x, ls, spell(rng, ls, s, n, kd, pool, p), s, n, th, wt)
def setup_inputs_corners(rng):
    kd, pool, x, ls, s, n, th, wt = parts(rng); sh = (N, 8, L)
    ls = np.where(rng.random(ls.shape) < 0.2, rng.choice(np.array([0, V - 1]), ls.shape), ls)
    edge = np.array(sorted({0, 1, 15, 16} | {2 * h - 2 for h in HS} | {2 * h - 1 for h in HS})); p = rng.choice(np.array(HS), sh); u = rng.random(sh)
    n = np.where(u < 0.4, 2 * p - 2, np.where(u < 0.7, 2 * p - 1, rng.choice(edge, sh)))
    n[0, 0] = 0; n[N - 1, 7] = 16; n[:, 3] = rng.choice(np.array([0, 16]), (N, L))
    s = np.where(rng.random(sh) < 0.3, rng.choice(np.array([0, 15, 16, 4095]), sh), s)
    th = rng.choice(np.array([0, 1, 20, 240]), (N, 8)); wt = rng.choice(np.array([0, 1, 255]), (N, 8, 16))
    p[N - 1, 7] = 8; th[N - 1, 7] = 0
    c = int(rng.integers(1, N - 1))
    x[c] = 8 * (np.arange(V) & 1) + rng.integers(0, 3, (8, 16, V)); th[c] = 8; th[c - 1] = 240
    ls[c - 1] |= 1; ls[c] -= ls[c] & 1
    n[c - 1] = 0; n[c] = np.maximum(n[c], 1); n[c, 7, L - 1] = 0
    a = pushed(ls, s, n); u = rng.integers(0, 4, sh); own = P * np.arange(L) + rng.integers(0, P, sh)
    b = np.where(u == 0, 0, np.where(u == 1, V - 1, np.where(u == 2, own, rng.integers(0, V, sh))))
    w = two(a, b, p); w[c, :, 0] = a[c]
    return pack(x, ls, w, s, n, th, wt)
def setup_inputs_ties(rng):
    kd, pool, x, ls, s, n, th, wt = parts(rng); sh = (N, 8, L); half = V >> 3
    th = rng.integers(16, 61, (N, 8)); val = np.stack([0 * th, th, th + 1, 2 * th + 1], -1)
    loose = np.ones(V, np.int64); loose[pool[:, :half]] = 0
    e = val[:, :, kd] + loose * rng.integers(0, 17, (N, 8, V)); x = (e[:, :, None] + np.arange(16)[:, None]) >> 4
    ls = np.where(rng.random(ls.shape) < 0.8, pool[rng.integers(0, 4, ls.shape), rng.integers(0, half, ls.shape)], ls)
    p = rng.choice(np.array(HS), sh); a = kd[pushed(ls, s, n)]; b = np.array([3, 3, 0, 0])[a]
    c = np.where(rng.random(sh) < 0.6, np.array([1, 0, 3, 2])[a], np.array([2, 3, 0, 1])[a])
    k = np.where(np.arange(1, 17)[:, None] == p[:, :, None], c[:, :, None], two(a, b, p))
    return pack(x, ls, pool[k, rng.integers(0, half, k.shape)], s, n, th, wt)
def setup_inputs_again(rng):
    kd, pool, x, ls, s, n, th, wt = parts(rng)
    few = np.concatenate([np.arange(4 * P), V - 4 * P + np.arange(4 * P)])
    x = np.clip(rng.integers(0, 16, (N, 8, 16, 1)) + rng.integers(-3, 4, (N, 8, 16, V)), 0, 15); th = rng.integers(24, 44, (N, 8))
    ls = few[rng.integers(0, 8 * P, ls.shape)]; w = few[rng.integers(0, 8 * P, (N, 8, 16, L))]
    q = int(rng.integers(0, N)); n[q] = np.maximum(n[q], 1); w[q, :, 0] = pushed(ls, s, n)[q]
    return pack(x, ls, w, s, n, th, wt)
def setup_inputs_spread(rng):
    sh = (N, 8, L)
    x = np.minimum((np.exp2(4 * rng.random((N, 8, 1, V))) * rng.random((N, 8, 16, V))).astype(np.int64), 15)
    ls = np.minimum((V * rng.random((N, 8, 16, M)) * np.sqrt(rng.random((N, 8, 16, M)))).astype(np.int64), V - 1)
    w = np.minimum((np.exp2(np.log2(V) * rng.random((N, 8, 16, L)))).astype(np.int64), V - 1)
    s = np.where(rng.random(sh) < 0.5, rng.integers(0, 4096, sh), np.minimum(np.exp2(12 * rng.random(sh)).astype(np.int64), 4095))
    wt = np.minimum(np.exp2(8 * rng.random((N, 8, 16))).astype(np.int64) - 1, 255)
    return pack(x, ls, w, s, rng.integers(0, 17, sh), rng.integers(0, 241, (N, 8)), wt)
def setup_inputs_ends(rng):
    sh = (N, 8, L)
    u = rng.integers(0, 3, (N, 8, 1, V)); x = 15 * np.where(u == 2, rng.integers(0, 2, (N, 8, 16, V)), u)
    x[:, 1:7:2, :, 0] = 0; x[:, 1:7:2, :, V - 1] = 15; x[:, 7, :, 0] = 0; x[:, 7, :, V - 1] = 15; x[:, 0, :, 0] = 15; x[:, 0, :, V - 1] = 0
    ls = (V - 1) * rng.integers(0, 2, (N, 8, 16, M)); s = 4095 * rng.integers(0, 2, sh); n = 16 * (rng.random(sh) < 0.75).astype(np.int64)
    th = 240 * rng.integers(0, 2, (N, 8)); th[:, 7] = 0; th[:, 6] = 240
    wt = 255 * rng.integers(0, 2, (N, 8, 16)); wt[:, 7] = 255; wt[:, 0] = 0
    p = rng.choice(np.array((0,) + HS), sh)
    for i, k in ((0, 0), (1, 8), (7, 0), (10, 8), (L - 2, 8), (L - 1, 0)):
        s[:, 7, i] = 4095; n[:, 7, i] = 16; p[:, 7, i] = k
    ls[:, 7, 15, ((4095 * 4095 >> 5) + 4095 + 77 * 16) & (M - 1)] = V - 1
    a = pushed(ls, s, n)
    return pack(x, ls, two(a, V - 1 - a, p), s, n, th, wt)
def check_inputs(d):
    bad = []
    for k, lo, hi in (("x", 0, 15), ("ls", 0, V - 1), ("wd", 0, V - 1), ("nl", 0, 16), ("sd", 0, 4095), ("th", 0, 240), ("wt", 0, 255)):
        v = np.asarray(d[k]).astype(np.float64)
        if not np.all((v >= lo) & (v <= hi)): bad.append("range of " + k)
        if not np.all(v == np.floor(v)): bad.append("whole numbers in " + k)
    w = np.asarray(d["wd"]).reshape(N, 8, 16, L); n = np.asarray(d["nl"]).reshape(N, 8, 1, L)
    if np.any((np.arange(16)[:, None] >= n) & (w != 0)): bad.append("empty rows of wd")
    return bad
def reference(x, ls, wd, nl, sd, th, wt):
    X = x.astype(np.float32).astype(np.int32).reshape(N, 8, 16, V); tab = ls.astype(np.int64).reshape(N, 8, 16 * M)
    w = wd.astype(np.int64).reshape(N, 8, 16, L); n = nl.astype(np.int64); s = sd.astype(np.int64)
    lim = th.astype(np.int64).reshape(N, 8, 1, 1); wgt = wt.astype(np.int64).reshape(N, 8, 16, 1)
    A = np.zeros(N, np.int64); row = np.arange(16)[:, None]
    for t in range(TV):
        new = np.take_along_axis(tab, (s & 15) * M + (((s * s >> 5) + s + 77 * n) & (M - 1)), 2)
        w = np.concatenate([new[:, :, None], w[:, :, :15]], axis=2); n = np.minimum(n + 1, 16)
        G = np.take_along_axis(X, w.reshape(N, 8, 1, 16 * L), 3).reshape(N, 8, 16, 16, L)
        bound = lim + (A & 15).reshape(N, 1, 1, 1); h = np.zeros((N, 8, L), np.int64)
        for k in HS:
            D = np.add.reduce(np.abs(G[:, :, :, :k] - G[:, :, :, k:2 * k]), axis=2)
            h = np.where((h == 0) & (2 * k <= n) & np.all(D <= bound, axis=2), k, h)
        hit = h > 0
        z = np.maximum.reduce(np.where(row < h[:, :, None, None, :], G, 0), axis=3)
        tot = np.add.reduce(wgt * np.where(hit[:, :, None], z, G[:, :, :, 0]), axis=2)
        s = np.where(hit, tot + h, 5 * s + tot) & 4095
        at = row + h[:, :, None, :]
        w = np.where(at < 16, np.take_along_axis(w, np.minimum(at, 15), 2), 0); n = n - h
        col = np.roll(P * np.arange(L) + (s & (P - 1)), 1, axis=0)[:, :, None]
        old = np.take_along_axis(X, col, 3)
        val = np.where(np.roll(hit, 1, axis=0)[:, :, None], (old + np.roll(z, 1, axis=0)) >> 1, old)
        np.put_along_axis(X, col, val.astype(np.int32), 3)
        A = np.add.reduce(hit.astype(np.int64).reshape(N, 8 * L), axis=1)
        if t < TV - 1:
            by = 1 + (t + 1) // N - t // N
            w, n, s = [np.roll(np.roll(v, 1, axis=0), by, axis=1) for v in (w, n, s)]
    return {"yx": X.reshape(N, 128, V).astype(np.float32).astype(BF), "yw": w.reshape(N, 128, L).astype(np.float32), "yn": n.astype(np.float32), "ys": s.astype(np.float32)}

@@ -1,0 +1,561 @@
+from concourse.bass import DstId, RemoteDMATransfer
+from concourse.mybir import AluOpType as A, AxisListType, ActivationFunctionType as AF
+
+TV = 6
+BIG = 5.0 * 2.0 ** 22
+NX = 2304
+NH = 2064
+MATS = ("LOs", "LOq", "HIe", "HIo", "LOe", "LOo", "M1", "LOe0", "LOo0", "HIe0", "HIo0", "M10", "eye", "neg", "N0", "N1", "one")
+SCRATCH = {}
+for _t in range(TV):
+    SCRATCH["xb%d" % _t] = ("sbuf", [128, NX], "bfloat16")
+    SCRATCH["hl%d" % _t] = ("sbuf", [128, NH], "bfloat16")
+for _m in MATS:
+    SCRATCH[_m] = ("sbuf", [128, 128], "bfloat16")
+for _b in range(8):
+    SCRATCH["pb%d" % _b] = ("psum", [128, 512], "float32")
+for _n, _w, _d in (
+        ("xf", NX, "bfloat16"), ("xr", 2048, "bfloat16"), ("lsi", 1024, "int32"), ("lsH", 1024, "bfloat16"), ("lsL", 1024, "bfloat16"),
+        ("TL", 16384, "bfloat16"), ("win", 2560, "bfloat16"), ("whl", 512, "bfloat16"), ("wdi", 256, "int32"),
+        ("G", 2048, "bfloat16"), ("d8", 2048, "bfloat16"), ("P", 2048, "bfloat16"), ("RM", 2048, "bfloat16"), ("Zc", 1024, "bfloat16"),
+        ("ab13", 1024, "bfloat16"), ("SelH", 256, "bfloat16"), ("SelL", 256, "bfloat16"), ("R", 256, "bfloat16"),
+        ("ll", 128, "uint16"), ("lh", 128, "uint16"), ("zl", 16, "uint16"), ("col", 16, "uint16"), ("wl", 16, "uint16"), ("cl", 16, "uint16"),
+        ("zz", 256, "bfloat16"), ("oldh", 256, "bfloat16"), ("zf", 256, "bfloat16"), ("cf", 16, "uint16"),
+        ("roll", 128, "float32"), ("Q1", 144, "bfloat16"), ("QW", 144, "bfloat16"), ("rollb", 128, "bfloat16"),
+        ("dif", 128, "int32"), ("mi", 144, "int32"), ("pc", 1, "int32"), ("cI", 2, "int32"), ("cF", 16, "float32"),
+        ("bi", 16, "int32"), ("iB", 16, "int32"), ("i8", 16, "int32"), ("iBd", 16, "float32"),
+        ("KT", 64, "float32"), ("TAGC", 64, "float32"), ("TAG", 64, "float32"),
+        ("s4", 64, "int32"), ("sq", 64, "int32"), ("u", 64, "int32"), ("f", 64, "int32"), ("cand", 64, "float32"),
+        ("c13", 64, "float32"), ("e13", 32, "float32"), ("E", 16, "float32"), ("M8", 128, "float32"), ("c8", 16, "float32"),
+        ("SF", 16, "float32"), ("SI", 16, "int32"), ("SrI", 16, "int32"), ("k1", 16, "int32"), ("k2", 16, "int32"), ("k3", 16, "int32"),
+        ("kf", 16, "float32"), ("sI", 16, "int32"), ("nF", 16, "float32"), ("f1", 16, "bfloat16"), ("f2", 16, "bfloat16"), ("f3", 16, "bfloat16"),
+        ("npb", 16, "bfloat16"), ("Bc", 1, "float32"), ("aI", 1, "int32"), ("amo", 16, "int32"), ("ami", 16, "int32"),
+        ("CH", 128, "bfloat16"), ("e77", 128, "bfloat16"),
+        ("nsd", 512, "int32"), ("src8", 768, "bfloat16"), ("e8", 144, "bfloat16"), ("br", 128, "bfloat16"), ("ebig", 128, "bfloat16"),
+        ("thi", 1, "int32"), ("thb", 1, "bfloat16"), ("wti", 1, "int32"),
+        ("IND", 32, "float32"), ("m4", 128, "int32"), ("hs", 256, "float32"), ("yws", 256, "float32"), ("ywr", 256, "float32"),
+        ("nst", 32, "float32"), ("nsx", 32, "float32"), ("nsr", 32, "float32"), ("xo", 2048, "bfloat16")):
+    SCRATCH[_n] = ("sbuf", [128, _w], _d)
+SCRATCH["ab8"] = ("sbuf", [128, 16, 128], "bfloat16")
+
+RING = ["x%d" % t for t in range(1, TV)] + ["h%d" % t for t in range(1, TV)] + ["a%d" % t for t in range(1, TV)]
+FIN = ["xf", "zf", "cf", "yf", "nf"]
+SEMAPHORES = (["V", "S", "P", "G", "L", "q"] + ["r_" + n for n in RING + FIN] + ["tl%d" % t for t in range(TV)] + ["tlb", "tlc"] + ["wi%d" % t for t in range(TV)]
+              + ["i_" + n for n in ("x", "ls", "wd", "ns", "th", "wt")] + ["o_" + n for n in ("x0", "x1", "w", "ns", "nt")])
+
+
+def message(name):
+    if name in FIN:
+        return {"xf": (-5, "xb5", "xf", 256, 2048, 4, 0), "zf": (-6, "zz", "zf", 0, 256, 1, 0), "cf": (-6, "col", "cf", 0, 16, 1, 1),
+                "yf": (-5, "yws", "ywr", 0, 256, 1, 2), "nf": (-5, "nsx", "nsr", 0, 32, 1, 3)}[name]
+    t = int(name[1:])
+    return {"x": (1, "xb%d" % (t - 1), "xb%d" % t, 256, 2048, 4, 0), "h": (1, "hl%d" % (t - 1), "hl%d" % t, 0, NH, 4, 0),
+            "a": (1, "amo", "ami", 2 * t, 2, 1, 1)}[name[0]]
+
+
+def order():
+    o = ["x1", "h1", "h2"]
+    for t in range(1, TV):
+        o.append("a%d" % t)
+        o.append("x%d" % (t + 1) if t + 1 < TV else "xf")
+        if t + 2 < TV:
+            o.append("h%d" % (t + 2))
+    return o + ["zf", "cf", "yf", "nf"]
+
+
+def route(name, src, dst, topo):
+    _, _, _, c0, w, pieces, first = message(name)
+    if topo.may_write(src, dst):
+        return [(None, c0, w)]
+    hs = [h for h in topo.cores_of(src) if topo.may_write(h, dst)]
+    hs = [h for h in hs if topo.die(h) == topo.die(src)] + [h for h in hs if topo.die(h) != topo.die(src)]
+    pieces = min(pieces, len(hs))
+    pick = hs[first % len(hs):] + hs[:first % len(hs)]
+    return [(pick[j], c0 + w // pieces * j, w // pieces) for j in range(pieces)]
+
+
+def peer(name, rank):
+    return (rank - message(name)[0]) % 8
+
+
+def put(g, T, topo, core, dst, sem, out, in_):
+    rid, pid = topo.addr(dst, core)
+    g.remote_dma(out, in_, T.sem[sem], T.sem.L, pid, rid, topo.mask(core, dst))
+    return len(topo.engines(core, dst))
+
+
+def helper_program(g, core, T, topo):
+    sent = 0
+    for name in order():
+        for r in range(8):
+            src, dst = T.cores[r], T.cores[peer(name, r)]
+            way = route(name, src, dst, topo)
+            for h, c0, w in way:
+                if h == core:
+                    buf = T[message(name)[2]]
+                    g.wait_ge(T.sem["r_" + name], len(topo.engines(src, core)) // len(way))
+                    sent += put(g, T, topo, core, dst, "r_" + name, buf[:, c0:c0 + w], buf[:, c0:c0 + w])
+    if sent:
+        g.wait_ge(T.sem.L, sent)
+
+
+def rank_program(g, core, T, topo):
+    rank = T.rank_of(core)
+    if rank is None:
+        return helper_program(g, core, T, topo)
+    Q = {"V": g.vector, "S": g.scalar, "P": g.tensor, "G": g, "Y": g.sync}
+    cnt, seen, last, read, bank = {q: 0 for q in Q}, {q: {} for q in Q}, {}, {}, {}
+    total = {}
+
+    def need(q, tok):
+        sem, val = tok[0], tok[1]
+        if seen[q].get(sem, 0) < val:
+            Q[q].wait_ge(T.sem[sem], val)
+            seen[q][sem] = val
+
+    def deps(q, R, W, B, dma):
+        for k in R:
+            if k in last:
+                need(q, last[k])
+        for k in W:
+            for tok in ([last[k]] if k in last else []) + list(read.get(k, {}).values()):
+                need(q, tok)
+        for b in B:
+            for q2, tok in bank.get(b, {}).items():
+                if q2 != q:
+                    need(q, tok)
+
+    def note(q, tok, R, W, B):
+        for k in W:
+            last[k] = tok
+            read[k] = {}
+        for k in R:
+            if k not in W:
+                read.setdefault(k, {})[(tok[2], tok[0])] = tok
+        for b in B:
+            bank.setdefault(b, {})[q] = tok
+
+    def run(q, call, R=(), W=(), B=()):
+        deps(q, R, W, B, False)
+        cnt[q] += 1
+        call().then_inc(T.sem[q], 1)
+        total[q] = cnt[q]
+        note(q, (q, cnt[q], q), R, W, B)
+
+    def dma(q, sem, pairs, R=(), W=()):
+        deps(q, R, W, (), True)
+        for out, in_ in pairs:
+            Q[q].dma_start(out, in_).then_inc(T.sem[sem], 16)
+            total[sem] = total.get(sem, 0) + 16
+        note(q, (sem, total[sem], None), R, W, ())
+
+    sent = [0]
+
+    def send(name, R):
+        dst = T.cores[peer(name, rank)]
+        sb, db = message(name)[1:3]
+        deps("G", R, (), (), True)
+        way = route(name, core, dst, topo)
+        if len(way) == 1:
+            h, c0, w = way[0]
+            sent[0] += put(g, T, topo, core, dst if h is None else h, "r_" + name, T[db][:, c0:c0 + w], T[sb][:, c0:c0 + w])
+            return
+        trs = []
+        for j, (h, c0, w) in enumerate(way):
+            es = topo.engines(core, h)
+            es = es[j * (len(es) // len(way)):(j + 1) * (len(es) // len(way))]
+            rid, pid = topo.addr(h, core)
+            trs.append(RemoteDMATransfer(dst_ids=[DstId(rid=rid, pnc=pid)], dma_engine_mask=sum(1 << e for e in es),
+                                         remote_sem=T.sem["r_" + name], srcs=[T[sb][:, c0:c0 + w]], dsts=[T[db][:, c0:c0 + w]]))
+            sent[0] += len(es)
+        g.remote_dma_fused(trs, local_sem=T.sem.L)
+
+    def landing(name, key):
+        src = T.cores[(rank + message(name)[0]) % 8]
+        n = 0
+        for h, _, _ in route(name, src, core, topo):
+            n += len(topo.engines(src if h is None else h, core))
+        last[key] = ("r_" + name, n, None)
+        read[key] = {}
+        total["r_" + name] = n
+
+    def ts(out, in0, s1, s2, op0, op1=None, R=(), W=(), B=()):
+        if op1 is None:
+            run("V", lambda: g.vector.tensor_scalar(out, in0, s1, None, op0), R, W, B)
+        else:
+            run("V", lambda: g.vector.tensor_scalar(out, in0, s1, s2, op0, op1), R, W, B)
+
+    def tt(out, a, b, op, R=(), W=(), B=()):
+        run("V", lambda: g.vector.tensor_tensor(out, a, b, op), R, W, B)
+
+    def cp(out, in_, R=(), W=(), B=()):
+        run("V", lambda: g.vector.tensor_copy(out, in_), R, W, B)
+
+    def fill(out, c, W, R=()):
+        run("V", lambda: g.vector.memset(out, c), R, W)
+
+    def act(out, in_, func=AF.Copy, R=(), W=(), B=(), **kw):
+        run("S", lambda: g.scalar.activation(out, in_, func, **kw), R, W, B)
+
+    def mm(out, l, r, start, stop, R=(), B=()):
+        run("P", lambda: g.tensor.matmul(out, l, r, start, stop), R, (), B)
+
+    def msum(out, bk, parts):
+        for j, (l, r, keys) in enumerate(parts):
+            mm(out, l, r, j == 0, j == len(parts) - 1, keys, (bk,))
+
+    dma("S", "i_ls", [(T.lsi[:], T.ls[:])], W=["lsi"])
+    dma("Y", "i_ns", [(T.nsd[0:8, 0:256], T.nl[:]), (T.nsd[0:8, 256:512], T.sd[:])], W=["nsd"])
+    dma("Y", "i_th", [(T.thi[0:8, :], T.th[:])], W=["thi"])
+    dma("Y", "i_wt", [(T.wti[:], T.wt[:])], W=["wti"])
+    dma("Y", "i_x", [(T.xr[:], T.x[:])], W=["xr"])
+    dma("Y", "i_wd", [(T.wdi[:], T.wd[:])], W=["wdi"])
+    run("G", lambda: g.iota(T.pc[:], [[0, 1]], 0, 1), (), ["pc"])
+    run("G", lambda: g.iota(T.dif[:], [[1, 128]], 256, -1), (), ["dif"])
+    run("G", lambda: g.iota(T.mi[:], [[1, 144]], 0, 0), (), ["mi"])
+    run("G", lambda: g.iota(T.bi[:], [[16, 16]], 0, 0), (), ["bi"])
+    run("G", lambda: g.iota(T.TL[:, 8192:10240], [[0, 2048]], 0, 0, allow_small_or_imprecise_dtypes=True), (), ["TLc"])
+    fill(T.TL[:, 0:2048], 0.0, ["TLa"])
+    fill(T.TL[:, 2048:8192], 0.0, ["TLd"])
+    for j in range(3):
+        act(T.TL[:, 10240 + 2048 * j:12288 + 2048 * j], T.TL[:, 0:2048], R=["TLa"], W=["TLb%d" % j])
+    act(T.xb0[:, 256:NX], T.xr[:], R=["xr"], W=["xb0"], bias=128.0)
+
+    cF = T.cF
+
+    def col(j):
+        return cF[:, j:j + 1]
+    ts(T.cI[:, 0:1], T.pc[:], 15, None, A.bitwise_and, R=["pc"], W=["cI"])
+    ts(T.cI[:, 1:2], T.pc[:], 112, None, A.bitwise_and, R=["pc"], W=["cI1"])
+    cp(cF[:, 0:2], T.cI[:], R=["cI", "cI1"], W=["c0"])
+    ts(T.dif[:], T.dif[:], 127, None, A.bitwise_and, R=["dif"], W=["dif"])
+    ts(col(3), col(0), 8.0, None, A.is_lt, R=["c0"], W=["c3"])
+    ts(col(4), col(0), 8.0, None, A.is_ge, R=["c0"], W=["c4"])
+
+    def mat(name, d, c):
+        ts(T[name][:], T.dif[:], float(d), col(c), A.is_equal, A.mult, R=["dif", "c%d" % c], W=[name])
+    mat("LOs", 0, 3)
+    mat("LOq", 8, 3)
+    mat("HIe", 120, 4)
+    mat("HIo", 0, 4)
+    cp(T.lsH[:], T.lsi[:], R=["lsi"], W=["lsH"])
+    tt(T.lsL[:], T.lsi[:], T.lsH[:], A.subtract, R=["lsi", "lsH"], W=["lsL"])
+    zero = ["TLa", "TLb0", "TLb1", "TLb2", "TLc", "TLd"]
+    dma("Y", "tl0", [(T.TL[a::16, 1024 * a:1024 * a + 1024], T.lsH[a::16, :]) for a in range(16)], R=zero + ["lsH"], W=["TL"])
+    for q, sem, key, a0 in (("Y", "tlb", "TLx", 0), ("S", "tlc", "TLy", 8)):
+        dma(q, sem, [(T.TL[(a + 8) % 16::16, 1024 * a:1024 * a + 1024], T.lsL[a::16, :]) for a in range(a0, a0 + 8)],
+            R=zero + ["lsL"], W=[key])
+    cp(col(12), T.pc[:], R=["pc"], W=["c12"])
+    ts(T.m4[0:8, :], T.mi[0:8, 0:128], 4, None, A.logical_shift_right, R=["mi"], W=["m4"])
+    ts(T.br[0:8, :], T.m4[0:8, :], cF[0:8, 12:13], None, A.is_equal, R=["m4", "c12"], W=["br"])
+    cp(T.thb[0:8, :], T.thi[0:8, :], R=["thi"], W=["thb"])
+    mm(T.pb6[:, 0:1], T.br[0:8, :], T.thb[0:8, :], True, True, ["br", "thb"], (6,))
+    def staging(b, l1, l2):
+        for h in range(2):
+            o = 2 * b + h
+            sl = slice(512 * h, 512 * h + 512)
+            msum(T["pb%d" % o][:, 0:512], o, [(T[l1][:], T.lsH[:, sl], [l1, "lsH"]), (T[l2][:], T.lsL[:, sl], [l2, "lsL"])])
+            act(T.hl0[:, 512 * o:512 * o + 512], T["pb%d" % o][:, 0:512], W=["hl0_%d" % o], B=(o,))
+    staging(0, "LOs", "LOq")
+    ts(col(11), T.pc[:], 16.0, 15.0, A.mult, A.add, R=["pc"], W=["c11"])
+    ts(T.e8[0:8, :], T.mi[0:8, :], cF[0:8, 11:12], None, A.is_equal, R=["mi", "c11"], W=["e8"])
+    cp(T.src8[0:8, 0:512], T.nsd[0:8, :], R=["nsd"], W=["src8"])
+    tt(T.src8[0:8, 512:768], T.nsd[0:8, 256:512], T.src8[0:8, 256:512], A.subtract, R=["nsd", "src8"], W=["src8b"])
+    msum(T.pb7[:, 0:48], 7, [(T.e8[0:8, 15 - a:143 - a], T.src8[0:8, a:768:16], ["e8", "src8", "src8b"]) for a in range(16)])
+    staging(1, "HIo", "HIe")
+
+    def sfill(out, c, key):
+        n = out.shape[1]
+        act(out, T.xr[:, 0:n], R=["xr"], W=[key], scale=0.0, bias=float(c))
+
+    def sfills():
+        sfill(T.RM[:], 1.0, "RM")
+        sfill(T.RM[:, 0:2048:8], 0.0, "RM")
+        sfill(T.one[:], 1.0, "one")
+        sfill(T.win[:, 1536:2048], 0.0, "win3")
+    sfill(T.CH[:], 0.0, "CH")
+    for j, (h, v) in enumerate(((1, -2.0 ** 24), (3, -2.0 ** 24 + 2.0 ** 22), (8, -2.0 ** 24 + 2.0 ** 23), (0, 0.0))):
+        sfill(T.TAGC[:, 16 * j:16 * j + 16], v, "TAGC")
+        if h:
+            sfill(T.KT[:, 16 * j:16 * j + 16], h, "KT")
+            sfill(T.CH[:, 16 * j:16 * j + 16], 2.0 * h * BIG + v, "CH")
+            sfill(T.CH[:, 64 + 16 * j:80 + 16 * j], -77.0 * h, "CH")
+    fill(T.hl0[:, 2050:NH], 0.0, ["hl0"])
+    cp(T.hl0[:, 2048:2049], T.wti[:], R=["wti"], W=["hl0w"])
+    cp(T.hl0[:, 2049:2050], T.pb6[:, 0:1], W=["hl0h"], B=(6,))
+    HL0 = ["hl0", "hl0w", "hl0h"] + ["hl0_%d" % o for o in range(4)]
+    ts(col(2), col(1), 15.0, None, A.add, R=["c0"], W=["c2"])
+    ts(col(6), col(0), 1.0, None, A.is_ge, R=["c0"], W=["c6"])
+    ts(col(7), col(0), 7.0, None, A.is_lt, R=["c0"], W=["c7"])
+    ts(col(9), col(0), 15.0, None, A.is_lt, R=["c0"], W=["c9"])
+    tt(col(5), col(6), col(3), A.mult, R=["c6", "c3"], W=["c5"])
+    tt(col(8), col(9), col(7), A.subtract, R=["c9", "c7"], W=["c8"])
+
+    def places0():
+        ts(T.k2[:], T.sI[:], 15, None, A.bitwise_and, R=["sI"], W=["k2"])
+        tt(T.k1[:], T.sI[:], T.sI[:], A.mult, R=["sI"], W=["k1"])
+        ts(T.k1[:], T.k1[:], 5, None, A.logical_shift_right, R=["k1"], W=["k1"])
+        tt(T.k1[:], T.k1[:], T.sI[:], A.add, R=["k1", "sI"], W=["k1"])
+        ts(T.k3[:], T.nF[:], 77.0, None, A.mult, R=["nF"], W=["k3"])
+        tt(T.k1[:], T.k1[:], T.k3[:], A.add, R=["k1", "k3"], W=["k1"])
+        ts(T.k1[:], T.k1[:], 1023, None, A.bitwise_and, R=["k1"], W=["k1"])
+        ts(T.k2[:], T.k2[:], 1024.0, None, A.mult, R=["k2"], W=["k2"])
+        tt(T.k1[:], T.k1[:], T.k2[:], A.add, R=["k1", "k2"], W=["k1"])
+        cp(T.cl[:], T.k1[:], R=["k1"], W=["cl"])
+        cp(T.SelH[:], T.wdi[:], R=["wdi"], W=["SelH"])
+        tt(T.SelL[:], T.wdi[:], T.SelH[:], A.subtract, R=["wdi", "SelH"], W=["SelL"])
+        mat("LOe0", 1, 7)
+        mat("LOo0", 9, 7)
+        ts(T.N0[:], T.mi[:, 0:128], col(1), None, A.is_equal, R=["mi", "c0"], W=["N0"])
+        ts(T.N1[:], T.mi[:, 0:128], 8.0, col(1), A.subtract, A.is_equal, R=["mi", "c0"], W=["N1"])
+        mat("HIe0", 121, 8)
+        mat("HIo0", 1, 8)
+
+    def rest():
+        ts(T.eye[:], T.dif[:], 0.0, None, A.is_equal, R=["dif"], W=["eye"])
+        ts(T.neg[:], T.dif[:], 0.0, -1.0, A.is_equal, A.mult, R=["dif"], W=["neg"])
+        mat("M10", 1, 9)
+        ts(T.npb[:], T.nF[:], 1.0, 16.0, A.add, A.min, R=["nF"], W=["npb"])
+        ts(T.ebig[:], T.dif[:], 0.0, -BIG, A.is_equal, A.mult, R=["dif"], W=["ebig"])
+        ts(T.e77[:], T.dif[:], 0.0, 77.0, A.is_equal, A.mult, R=["dif"], W=["e77"])
+        ts(T.KT[:, 48:64], T.sI[:], 5.0, None, A.mult, R=["sI"], W=["KT3"])
+        ts(T.Q1[:], T.mi[:], col(2), None, A.is_equal, R=["mi", "c2"], W=["Q1"])
+
+    def last_consts():
+        ts(T.iB[:], T.bi[:], col(0), None, A.add, R=["bi", "c0"], W=["iB"])
+        ts(T.i8[:], T.iB[:], 8.0, 256.0 - 16384.0, A.mult, A.add, R=["iB"], W=["i8"])
+        ts(T.iBd[:], T.iB[:], 1.0 / 512, None, A.mult, R=["iB"], W=["iBd"])
+        ts(T.roll[:], T.dif[:], 16.0, None, A.is_equal, R=["dif"], W=["roll"])
+        ts(T.rollb[:], T.dif[:], 16.0, None, A.is_equal, R=["dif"], W=["rollb"])
+        mat("LOe", 0, 5)
+        mat("LOo", 8, 5)
+        mat("M1", 0, 6)
+        fill(T.amo[:], 0, ["amo"])
+    cp(T.nF[:], T.pb7[:, 0:16], W=["nF"], B=(7,))
+    cp(T.sI[:], T.pb7[:, 16:32], W=["sI"], B=(7,))
+    tt(T.sI[:], T.pb7[:, 32:48], T.sI[:], A.add, R=["sI"], W=["sI"], B=(7,))
+    places0()
+
+    def table(t):
+        hl = T["hl%d" % t]
+        dma("Y", "tl%d" % t, [(T.TL[p::8, 1024 * (p + 8 * j):1024 * (p + 8 * j) + 1024], hl[p::8, 1024 * j:1024 * j + 1024])
+                              for p in range(8) for j in range(2)],
+            R=["hl%d" % t], W=["TL", "TLx", "TLy"])
+    send("x1", ["xb0", "TL"])
+    send("h1", HL0)
+    for t in range(1, TV):
+        landing("x%d" % t, "xb%d" % t)
+        landing("h%d" % t, "hl%d" % t)
+        landing("a%d" % t, "am%d" % t)
+    for n, k in (("xf", "xf"), ("zf", "zf"), ("cf", "cf"), ("yf", "ywr"), ("nf", "nsr")):
+        landing(n, k)
+
+    PAIRS = ((0, 1), (0, 3), (1, 4), (2, 5))
+
+    def squares():
+        ts(T.f1[:], T.SF[:], 0.0, -8.0, A.is_lt, A.mult, R=["SF"], W=["f1"])
+
+    def lengths(where):
+        msum(T.pb2[:, 0:16], 2, [(T[where][:], T[k][:], [where, k]) for k in ("npb", "f1", "f2", "f3")])
+
+    for t in range(TV):
+        end = t == TV - 1
+        xb, kx = T["xb%d" % t], ["xb%d" % t]
+        x = xb[:, 256:NX]
+        hl, kh = T["hl%d" % t], HL0 if t == 0 else ["hl%d" % t]
+        LE, LO_, HE, HO, MW = ("LOe0", "LOo0", "HIe0", "HIo0", "M10") if t == 0 else ("LOe", "LOo", "HIe", "HIo", "M1")
+        act(T.R[:], T.TL[:].indirect(T.cl[:]), R=["TL", "TLx", "TLy", "cl"], W=["R"])
+        if t == 0:
+            sfills()
+        if t:
+            act(T.SelH[:], T.win[:].indirect(T.wl[:]), R=["win", "win3", "wl"], W=["SelH"])
+            act(T.SelL[:], T.win[:, 256:2560].indirect(T.wl[:]), R=["win", "win3", "wl"], W=["SelL"])
+        ev, od = slice(0, 256, 2), slice(1, 256, 2)
+        msum(T.pb5[:, 0:128], 5, [(T.N0[:], T.R[:, ev], ["N0", "R"]), (T.N1[:], T.R[:, od], ["N1", "R"]),
+                                  (T[LE][:], T.SelH[:, ev], [LE, "SelH"]), (T[LO_][:], T.SelH[:, od], [LO_, "SelH"]),
+                                  (T[LE][:], T.SelL[:, ev], [LE, "SelL"]), (T[LO_][:], T.SelL[:, od], [LO_, "SelL"])])
+        msum(T.pb6[:, 0:128], 6, [(T[HE][:], T.SelH[:, ev], [HE, "SelH"]), (T[HO][:], T.SelH[:, od], [HO, "SelH"]),
+                                  (T[HE][:], T.SelL[:, ev], [HE, "SelL"]), (T[HO][:], T.SelL[:, od], [HO, "SelL"])])
+        cp(T.ll[:], T.pb5[:, 0:128], W=["ll"], B=(5,))
+        cp(T.lh[:], T.pb6[:, 0:128], W=["lh"], B=(6,))
+        if t == 0:
+            rest()
+        msum(T.pb7[:, 0:256], 7, [(T.N0[:], T.R[:], ["N0", "R"]), (T[MW][:], T.SelH[:], [MW, "SelH"]), (T[MW][:], T.SelL[:], [MW, "SelL"])])
+        if t:
+            lengths("rollb")
+            ts(T.KT[:, 48:64], T.sI[:], 5.0, None, A.mult, R=["sI"], W=["KT3"])
+        def gs(c):
+            s = slice(512 * c, 512 * c + 512)
+            tt(T.d8[:, s], x.indirect(T.lh[:, 32 * c:32 * c + 32]), T.G[:, s], A.subtract, R=kx + ["lh", "G%d" % c], W=["d8_%d" % c])
+        for c in range(4):
+            if c == 0:
+                act(T.G[:, 0:256], x.indirect(T.ll[:, 0:16]), R=kx + ["ll"], W=["Ga"])
+                act(T.G[:, 256:512], x.indirect(T.ll[:, 16:32]), R=kx + ["ll"], W=["G0"])
+            else:
+                act(T.G[:, 512 * c:512 * c + 512], x.indirect(T.ll[:, 32 * c:32 * c + 32]), R=kx + ["ll"], W=["G%d" % c])
+            if c == 0:
+                ts(T.QW[:], T.Q1[:], hl[:, 2048:2049], None, A.mult, R=["Q1"] + kh, W=["QW"])
+                tt(T.d8[:, 0:256], x.indirect(T.lh[:, 0:16]), T.G[:, 0:256], A.subtract, R=kx + ["lh", "Ga"], W=["d8_a"])
+                tt(T.d8[:, 256:512], x.indirect(T.lh[:, 16:32]), T.G[:, 256:512], A.subtract, R=kx + ["lh", "G0"], W=["d8_0"])
+            elif c < 3:
+                gs(c)
+            if c == 1:
+                act(T.whl[:, 0:256], T.pb7[:, 0:256], W=["wH"], B=(7,))
+                tt(T.whl[:, 256:512], T.pb7[:, 0:256], T.whl[:, 0:256], A.subtract, R=["wH"], W=["wL"], B=(7,))
+            for p, (i, j) in enumerate(PAIRS):
+                o = T["pb%d" % (p // 2)][:, 256 * (p % 2) + 64 * c:256 * (p % 2) + 64 * c + 64]
+                msum(o, p // 2, [(T.eye[:], T.G[:, 512 * c + i:512 * c + 512:8], ["eye", "G%d" % c]),
+                                 (T.neg[:], T.G[:, 512 * c + j:512 * c + 512:8], ["neg", "G%d" % c])])
+        w, W2 = T.win, T.whl
+        mv = []
+        for blk, h in ((0, 1), (1, 3), (2, 8), (4, 0)):
+            o = slice(512 * blk, 512 * blk + 512)
+            if end:
+                mv.append((w[0:128 - h, o], W2[h:128, :]))
+            else:
+                d = 17 - h
+                mv += [(w[d:128, o], W2[0:128 - d, :]), (w[0:d, o], W2[128 - d:128, :])]
+        dma("Y", "wi%d" % t, mv, R=["wH", "wL"], W=["win"])
+        if not end:
+            table(t + 1)
+        if t == 0:
+            g.sync.sem_inc(T.sem.q, 1)
+            total["q"] = 1
+            need("G", ("q", 1))
+            send("h2", ["hl1"])
+        if t and t + 2 < TV:
+            send("h%d" % (t + 2), ["hl%d" % (t + 1), "win"])
+
+        if t:
+            ts(T.npb[:], T.pb2[:, 0:16], 1.0, 16.0, A.add, A.min, W=["npb"], B=(2,))
+        mm(T.pb6[:, 128:256], T.eye[:], T.CH[:], True, False, ["eye", "CH"], (6,))
+        for j in range(8):
+            mm(T.pb6[:, 128 + 16 * j:144 + 16 * j], T["ebig" if j < 4 else "e77"][:], T.npb[:], False, j == 7, ["ebig", "e77", "npb"], (6,))
+        run("V", lambda: g.vector.tensor_tensor_scan(T.P[:], T.RM[:], T.G[:], 0.0, A.mult, A.max), ["RM", "G0", "G1", "G2", "G3"], ["P"])
+        tt(T.TAG[:], T.pb6[:, 128:192], T.TAGC[:], A.max, R=["TAGC"], W=["TAG"], B=(6,))
+        for s, e in enumerate((0, 2, 7, 0)):
+            ts(T.Zc[:, 256 * s:256 * s + 256], T.P[:, e:2048:8], -128.0, None, A.add, R=["P"], W=["Zc%d" % s])
+        gs(3)
+        if t == 0:
+            last_consts()
+
+        def ab(c):
+            act(T.ab8[:, 4 * c:4 * c + 4, :], T.d8[:, 512 * c:512 * c + 512], AF.Abs, R=["d8_%d" % c], W=["ab8_%d" % c])
+
+        def d8sum(hf):
+            bk = (2, 5)[hf]
+            msum(T["pb%d" % bk][:, 0:64], bk, [(T.Q1[:, 15 - a:143 - a], T.ab8[:, 8 * hf:8 * hf + 8, 8 * a:8 * a + 8],
+                                                      ["Q1", "ab8_%d" % (2 * hf), "ab8_%d" % (2 * hf + 1)]) for a in range(16)])
+        ab(0)
+        ab(1)
+        d8sum(0)
+        for p in range(4):
+            act(T.ab13[:, 256 * p:256 * p + 256], T["pb%d" % (p // 2)][:, 256 * (p % 2):256 * (p % 2) + 256], AF.Abs, W=["ab13_%d" % p], B=(p // 2,))
+        ab(2)
+        ab(3)
+        tb = T.xf if end else T["xb%d" % (t + 1)]
+        sfill(tb[:, 0:256], 128.0, "xft" if end else "xt%d" % (t + 1))
+        zpart = (T.pb4[:, 0:64], 4, [(T.QW[:, 15 - a:143 - a], T.Zc[:, a:1024:16], ["QW", "Zc0", "Zc1", "Zc2", "Zc3"]) for a in range(16)])
+        msum(zpart[0], zpart[1], zpart[2])
+        msum(T.pb3[:, 0:64], 3, [(T.Q1[:, 15 - a:143 - a], T.ab13[:, a:1024:16], ["Q1"] + ["ab13_%d" % p for p in range(4)]) for a in range(16)])
+        d8sum(1)
+
+        if t:
+            tt(T.Bc[:], hl[:, 2049:2050], T.ami[:, 2 * t:2 * t + 1], A.add, R=kh + ["am%d" % t], W=["Bc"])
+        else:
+            cp(T.Bc[:], hl[:, 2049:2050], R=kh, W=["Bc"])
+        tt(T.s4[:], T.pb4[:, 0:64], T.KT[:], A.add, R=["KT", "KT3"], W=["s4"], B=(4,))
+        ts(T.s4[:], T.s4[:], 4095, None, A.bitwise_and, R=["s4"], W=["s4"])
+        tt(T.sq[:], T.s4[:], T.s4[:], A.mult, R=["s4"], W=["sq"])
+        ts(T.f[:], T.s4[:], 1024.0, None, A.mult, R=["s4"], W=["f"])
+        ts(T.sq[:], T.sq[:], 5, None, A.logical_shift_right, R=["sq"], W=["sq"])
+        tt(T.u[:], T.s4[:], T.pb6[:, 192:256], A.add, R=["s4"], W=["u"], B=(6,))
+        tt(T.cand[:], T.TAG[:], T.f[:], A.add, R=["TAG", "f"], W=["cand"])
+        tt(T.u[:], T.u[:], T.sq[:], A.add, R=["u", "sq"], W=["u"])
+        run("V", lambda: g.vector.tensor_tensor_scan(T.M8[:, 0:64], T.RM[:, 0:64], T.pb2[:, 0:64], 0.0, A.mult, A.max), ["RM"], ["M8"], (2,))
+        ts(T.u[:], T.u[:], 1023, None, A.bitwise_and, R=["u"], W=["u"])
+        ts(T.c13[:], T.pb3[:, 0:64], T.Bc[:], BIG, A.is_gt, A.mult, R=["Bc"], W=["c13"], B=(3,))
+        tt(T.cand[:], T.cand[:], T.u[:], A.add, R=["cand", "u"], W=["cand"])
+        tt(T.c13[:, 16:32], T.c13[:, 16:32], T.c13[:, 32:48], A.max, R=["c13"], W=["c13"])
+        tt(T.c13[:, 16:32], T.c13[:, 16:32], T.c13[:, 48:64], A.max, R=["c13"], W=["c13"])
+        run("V", lambda: g.vector.tensor_tensor_scan(T.M8[:, 64:128], T.RM[:, 0:64], T.pb5[:, 0:64], 0.0, A.mult, A.max), ["RM"], ["M8b"], (5,))
+        tt(T.e13[:], T.c13[:, 0:32], T.cand[:, 0:32], A.add, R=["c13", "cand"], W=["e13"])
+        ts(T.c8[:], T.M8[:, 7:128:8], T.Bc[:], BIG, A.is_gt, A.mult, R=["M8", "M8b", "Bc"], W=["c8"])
+        tt(T.E[:], T.e13[:, 0:16], T.e13[:, 16:32], A.min, R=["e13"], W=["E"])
+        tt(T.c8[:], T.c8[:], T.cand[:, 32:48], A.add, R=["c8", "cand"], W=["c8"])
+        tt(T.E[:], T.E[:], T.cand[:, 48:64], A.min, R=["E", "cand"], W=["E"])
+        tt(T.SI[:], T.c8[:], T.E[:], A.min, R=["c8", "E"], W=["SI"])
+        tt(T.SF[:], T.c8[:], T.E[:], A.min, R=["c8", "E"], W=["SF"])
+        ts(T.k1[:], T.SI[:], 14, 768, A.arith_shift_right, A.bitwise_and, R=["SI"], W=["k1"])
+        ts(T.k2[:], T.SI[:], 10, 7 + 16384, A.arith_shift_right, A.bitwise_and, R=["SI"], W=["k2"])
+        tt(T.k1[:], T.k1[:], T.iB[:], A.add, R=["k1", "iB"], W=["k1"])
+        tt(T.k2[:], T.k2[:], T.i8[:], A.add, R=["k2", "i8"], W=["k2"])
+        cp(T.zl[:], T.k1[:], R=["k1"], W=["zl"])
+        act(T.zz[:], T.Zc[:].indirect(T.zl[:]), R=["Zc0", "Zc1", "Zc2", "Zc3", "zl"], W=["zz"], scale=0.5, bias=31.75)
+        if not end:
+            mm(T.pb4[:, 0:16], T.roll[:], T.SF[:], True, True, ["roll", "SF"], (4,))
+        if end:
+            squares()
+            tt(T.k2[:], T.k2[:], T.iB[:], A.max, R=["k2", "iB"], W=["k2"])
+            cp(T.col[:], T.k2[:], R=["k2"], W=["col"])
+        else:
+            cp(T.SrI[:], T.pb4[:, 0:16], W=["SrI"], B=(4,))
+            ts(T.k3[:], T.SrI[:], 16383, None, A.bitwise_and, R=["SrI"], W=["k3"])
+            ts(T.sq[:, 0:16], T.SrI[:], 22, None, A.arith_shift_right, R=["SrI"], W=["sq"])
+            cp(T.cl[:], T.k3[:], R=["k3"], W=["cl"])
+            tt(T.kf[:], T.sq[:, 0:16], T.iBd[:], A.add, R=["sq", "iBd"], W=["kf"])
+            tt(T.k2[:], T.k2[:], T.iB[:], A.max, R=["k2", "iB"], W=["k2"])
+            ts(T.wl[:], T.kf[:], 512.0, 2048.0, A.mult, A.add, R=["kf"], W=["wl"])
+            cp(T.col[:], T.k2[:], R=["k2"], W=["col"])
+            squares()
+            mm(T.pb3[:, 0:16], T.one[:], T.f1[:], True, True, ["one", "f1"], (3,))
+            n = t + 1
+            xn = T["xb%d" % n]
+            ts(T.oldh[:], xn[:].indirect(T.col[:]), 0.5, 32.0, A.mult, A.add, R=["xb%d" % n, "xt%d" % n, "col"], W=["oldh"])
+            tt(xn[:].indirect(T.col[:]), T.oldh[:], T.zz[:], A.add, R=["oldh", "zz", "col"], W=["xb%d" % n])
+            run("V", lambda: g.vector.tensor_reduce(cF[:, 13:14], T.pb3[:, 0:16], AxisListType.X, A.add), (), ["asum"], (3,))
+            ts(T.f2[:], T.SF[:], -2.0 ** 23, 5.0, A.is_lt, A.mult, R=["SF"], W=["f2"])
+            ts(T.f3[:], T.SF[:], -3.0 * 2.0 ** 22, 2.0, A.is_lt, A.mult, R=["SF"], W=["f3"])
+            ts(T.aI[:], cF[:, 13:14], -0.125, None, A.mult, R=["asum"], W=["aI"])
+            ts(T.sI[:], T.SrI[:], 10, 4095, A.arith_shift_right, A.bitwise_and, R=["SrI"], W=["sI"])
+            ts(T.amo[:, 2 * n:2 * n + 1], T.aI[:], 15, None, A.bitwise_and, R=["aI", "amo"], W=["amo%d" % n])
+            send("a%d" % n, ["amo", "amo%d" % n])
+            send("x%d" % (n + 1) if n + 1 < TV else "xf", ["xb%d" % n])
+
+    send("zf", ["zz"])
+    send("cf", ["col"])
+    ts(T.f2[:], T.SF[:], -2.0 ** 23, 5.0, A.is_lt, A.mult, R=["SF"], W=["f2"])
+    ts(T.f3[:], T.SF[:], -3.0 * 2.0 ** 22, 2.0, A.is_lt, A.mult, R=["SF"], W=["f3"])
+    ts(T.sq[:, 0:16], T.SI[:], 22, None, A.arith_shift_right, R=["SI"], W=["sq"])
+    lengths("eye")
+    tt(T.kf[:], T.sq[:, 0:16], T.iBd[:], A.add, R=["sq", "iBd"], W=["kf"])
+    ts(T.k1[:], T.SI[:], 10, 4095, A.arith_shift_right, A.bitwise_and, R=["SI"], W=["k1"])
+    ts(T.wl[:], T.kf[:], 512.0, 2048.0, A.mult, A.add, R=["kf"], W=["wl"])
+    cp(T.cl[:], T.pb2[:, 0:16], W=["cl"], B=(2,))
+    act(T.SelH[:], T.win[:].indirect(T.wl[:]), R=["win", "win3", "wl"], W=["SelH"])
+    act(T.SelL[:], T.win[:, 256:2560].indirect(T.wl[:]), R=["win", "win3", "wl"], W=["SelL"])
+    ts(T.IND[:], T.mi[:, 0:32], col(0), None, A.is_gt, R=["mi", "c0"], W=["IND"])
+    cp(T.nst[:, 0:16], T.pb2[:, 0:16], W=["nst"], B=(2,))
+    cp(T.nst[:, 16:32], T.k1[:], R=["k1"], W=["nst2"])
+    run("V", lambda: g.vector.transpose(T.nsx[:], T.nst[:]), ["nst", "nst2"], ["nsx"])
+    tt(T.hs[:], T.SelH[:], T.SelL[:], A.add, R=["SelH", "SelL"], W=["hs"])
+    tt(T.yws[:], T.IND[:].indirect(T.cl[:]), T.hs[:], A.mult, R=["IND", "cl", "hs"], W=["yws"])
+    send("yf", ["yws"])
+    send("nf", ["nsx"])
+    ts(T.oldh[:], T.xf[:].indirect(T.cf[:]), 0.5, 32.0, A.mult, A.add, R=["xf", "xft", "cf"], W=["oldh"])
+    tt(T.xf[:].indirect(T.cf[:]), T.oldh[:], T.zf[:], A.add, R=["oldh", "zf", "cf"], W=["xf"])
+    ts(T.xo[:, 0:1280], T.xf[:, 256:1536], -128.0, None, A.add, R=["xf"], W=["xo0"])
+    act(T.xo[:, 1280:2048], T.xf[:, 1536:NX], R=["xf"], W=["xo1"], bias=-128.0)
+    ys = []
+    for a in range(4):
+        for b in range(2):
+            for k, y in enumerate((T.yn, T.ys)):
+                ys.append((y[2 * a + b:2 * a + b + 1, :], T.nsr[32 * a + 16 * k:32 * a + 16 * k + 16, 16 * b:16 * b + 16]))
+    dma("Y", "o_x0", [(T.yx[:, 0:1280], T.xo[:, 0:1280])], R=["xo0"])
+    dma("S", "o_x1", [(T.yx[:, 1280:2048], T.xo[:, 1280:2048])], R=["xo1"])
+    dma("Y", "o_w", [(T.yw[:], T.ywr[:])], R=["ywr"])
+    dma("Y", "o_ns", ys[0::2], R=["nsr"])
+    dma("S", "o_nt", ys[1::2], R=["nsr"])
+    for s in total:
+        need("Y", (s, total[s]))
+    g.wait_ge(T.sem.L, sent[0])

@@ -1,86 +1,90 @@
 from concourse.bass import DstId, RemoteDMATransfer
-from concourse.mybir import AluOpType as A, AxisListType, ActivationFunctionType as AF
+from concourse.mybir import AluOpType as A, ActivationFunctionType as AF
 
 TV = 6
-BIG = 5.0 * 2.0 ** 22
-NX = 2304
-NH = 2064
-MATS = ("LOs", "LOq", "HIe", "HIo", "LOe", "LOo", "M1", "LOe0", "LOo0", "HIe0", "HIo0", "M10", "eye", "neg", "N0", "N1", "one")
-SCRATCH = {}
+BIG = 1.0e20
+SC = 2.0 ** 20
+TAG = 17
+QW1, WTB, NTH, XW = 2048, 2192, 2224, 2240
+OFF = 15.5
+SCRATCH = {"XB": ("sbuf", [128, (TV + 1) * XW], "bfloat16")}
 for _t in range(TV):
-    SCRATCH["xb%d" % _t] = ("sbuf", [128, NX], "bfloat16")
-    SCRATCH["hl%d" % _t] = ("sbuf", [128, NH], "bfloat16")
-for _m in MATS:
+    SCRATCH["tb%d" % _t] = ("sbuf", [128, 1024], "int32")
+for _m in ("eye", "neg", "e8", "e2048", "n2464", "roll", "grp"):
     SCRATCH[_m] = ("sbuf", [128, 128], "bfloat16")
+for _m in ("N0", "N1", "LE", "LO", "HE", "HO", "MW"):
+    SCRATCH[_m] = ("sbuf", [128, 128], "float16")
+for _m in ("eye32", "n32", "roll32", "roll5", "one32"):
+    SCRATCH[_m] = ("sbuf", [128, 128], "float32")
 for _b in range(8):
     SCRATCH["pb%d" % _b] = ("psum", [128, 512], "float32")
 for _n, _w, _d in (
-        ("xf", NX, "bfloat16"), ("xr", 2048, "bfloat16"), ("lsi", 1024, "int32"), ("lsH", 1024, "bfloat16"), ("lsL", 1024, "bfloat16"),
-        ("TL", 16384, "bfloat16"), ("win", 2560, "bfloat16"), ("whl", 512, "bfloat16"), ("wdi", 256, "int32"),
-        ("G", 2048, "bfloat16"), ("d8", 2048, "bfloat16"), ("P", 2048, "bfloat16"), ("RM", 2048, "bfloat16"), ("Zc", 1024, "bfloat16"),
-        ("ab13", 1024, "bfloat16"), ("SelH", 256, "bfloat16"), ("SelL", 256, "bfloat16"), ("R", 256, "bfloat16"),
-        ("ll", 128, "uint16"), ("lh", 128, "uint16"), ("zl", 16, "uint16"), ("col", 16, "uint16"), ("wl", 16, "uint16"), ("cl", 16, "uint16"),
-        ("zz", 256, "bfloat16"), ("oldh", 256, "bfloat16"), ("zf", 256, "bfloat16"), ("cf", 16, "uint16"),
-        ("roll", 128, "float32"), ("Q1", 144, "bfloat16"), ("QW", 144, "bfloat16"), ("rollb", 128, "bfloat16"),
-        ("dif", 128, "int32"), ("mi", 144, "int32"), ("pc", 1, "int32"), ("cI", 2, "int32"), ("cF", 16, "float32"),
-        ("bi", 16, "int32"), ("iB", 16, "int32"), ("i8", 16, "int32"), ("iBd", 16, "float32"),
-        ("KT", 64, "float32"), ("TAGC", 64, "float32"), ("TAG", 64, "float32"),
-        ("s4", 64, "int32"), ("sq", 64, "int32"), ("u", 64, "int32"), ("f", 64, "int32"), ("cand", 64, "float32"),
-        ("c13", 64, "float32"), ("e13", 32, "float32"), ("E", 16, "float32"), ("M8", 128, "float32"), ("c8", 16, "float32"),
-        ("SF", 16, "float32"), ("SI", 16, "int32"), ("SrI", 16, "int32"), ("k1", 16, "int32"), ("k2", 16, "int32"), ("k3", 16, "int32"),
-        ("kf", 16, "float32"), ("sI", 16, "int32"), ("nF", 16, "float32"), ("f1", 16, "bfloat16"), ("f2", 16, "bfloat16"), ("f3", 16, "bfloat16"),
-        ("npb", 16, "bfloat16"), ("Bc", 1, "float32"), ("aI", 1, "int32"), ("amo", 16, "int32"), ("ami", 16, "int32"),
-        ("CH", 128, "bfloat16"), ("e77", 128, "bfloat16"),
-        ("nsd", 512, "int32"), ("src8", 768, "bfloat16"), ("e8", 144, "bfloat16"), ("br", 128, "bfloat16"), ("ebig", 128, "bfloat16"),
-        ("thi", 1, "int32"), ("thb", 1, "bfloat16"), ("wti", 1, "int32"),
-        ("IND", 32, "float32"), ("m4", 128, "int32"), ("hs", 256, "float32"), ("yws", 256, "float32"), ("ywr", 256, "float32"),
-        ("nst", 32, "float32"), ("nsx", 32, "float32"), ("nsr", 32, "float32"), ("xo", 2048, "bfloat16")):
-    SCRATCH[_n] = ("sbuf", [128, _w], _d)
-SCRATCH["ab8"] = ("sbuf", [128, 16, 128], "bfloat16")
+        ("xr", [2048], "bfloat16"), ("xo", [2048], "bfloat16"), ("wdi", [256], "int32"), ("win", [2304], "float32"),
+        ("G", [2048], "bfloat16"), ("d8", [2048], "bfloat16"), ("P", [2048], "bfloat16"), ("RM", [512], "bfloat16"),
+        ("ab8", [64, 32], "bfloat16"), ("ab13", [64, 16], "bfloat16"),
+        ("Sel", [256], "float16"), ("R", [256], "float16"), ("msk", [256], "bfloat16"), ("EQ", [16], "bfloat16"),
+        ("ll", [256], "uint16"), ("zl", [16], "uint16"), ("ol", [16], "uint16"), ("wa", [32], "uint16"), ("cc", [32], "uint16"), ("of", [16], "uint16"), ("cf", [16], "uint16"),
+        ("zz", [256], "bfloat16"), ("oldh", [256], "bfloat16"), ("zf", [256], "bfloat16"),
+        ("Q8", [144], "bfloat16"), ("dif", [128], "int32"), ("mi", [144], "int32"), ("pc", [1], "int32"), ("cI", [8], "int32"), ("cF", [24], "float32"),
+        ("jj", [16], "int32"), ("POS", [16], "float32"), ("CZ", [160], "bfloat16"), ("CY", [160], "bfloat16"), ("Z0", [128], "float32"),
+        ("MZ", [128], "float32"), ("M13", [16], "float32"), ("zF", [16], "float32"), ("hm", [16], "int32"), ("hw", [16], "int32"), ("I8", [16], "float32"),
+        ("M8", [128], "float32"), ("f13", [16], "float32"), ("F", [64], "float32"), ("DX", [160], "float32"), ("L", [160], "float32"),
+        ("I", [96], "int32"), ("pre", [32], "int32"), ("s32", [32], "int32"), ("tt", [32], "int32"), ("s7", [16], "int32"),
+        ("J", [16], "bfloat16"), ("J1", [16], "float32"), ("K", [32], "float32"), ("r15", [16], "bfloat16"), ("nb", [16], "bfloat16"), ("Bt", [128], "bfloat16"), ("ones", [208], "bfloat16"),
+        ("junk", [16], "float32"), ("cnt", [1], "float32"), ("Fs", [1], "float32"), ("rr", [1], "bfloat16"), ("amo", [8], "float32"), ("ami", [8], "float32"),
+        ("nsd", [512], "int32"), ("src8", [768], "bfloat16"), ("e8r", [144], "bfloat16"), ("br", [128], "bfloat16"),
+        ("thi", [1], "int32"), ("thb", [1], "bfloat16"), ("wti", [1], "int32"), ("m4", [128], "int32"),
+        ("IND", [32], "float32"), ("hs", [256], "float32"), ("yws", [256], "float32"), ("ywr", [256], "float32"),
+        ("nst", [32], "float32"), ("nsx", [32], "float32"), ("nsr", [32], "float32")):
+    SCRATCH[_n] = ("sbuf", [128] + _w, _d)
 
 RING = ["x%d" % t for t in range(1, TV)] + ["h%d" % t for t in range(1, TV)] + ["a%d" % t for t in range(1, TV)]
-FIN = ["xf", "zf", "cf", "yf", "nf"]
-SEMAPHORES = (["V", "S", "P", "G", "L", "q"] + ["r_" + n for n in RING + FIN] + ["tl%d" % t for t in range(TV)] + ["tlb", "tlc"] + ["wi%d" % t for t in range(TV)]
+FIN = ["xf", "zf", "of", "cf", "yf", "nf"]
+SEMAPHORES = (["V", "S", "P", "G", "L"] + ["r_" + n for n in RING + FIN] + ["wi%d" % t for t in range(TV)] + ["l%d" % t for t in range(TV)]
               + ["i_" + n for n in ("x", "ls", "wd", "ns", "th", "wt")] + ["o_" + n for n in ("x0", "x1", "w", "ns", "nt")])
+
+
+def slot(t):
+    return (TV - t) * XW
 
 
 def message(name):
     if name in FIN:
-        return {"xf": (-5, "xb5", "xf", 256, 2048, 4, 0), "zf": (-6, "zz", "zf", 0, 256, 1, 0), "cf": (-6, "col", "cf", 0, 16, 1, 1),
-                "yf": (-5, "yws", "ywr", 0, 256, 1, 2), "nf": (-5, "nsx", "nsr", 0, 32, 1, 3)}[name]
+        return {"xf": (-5, "XB", slot(5), "XB", slot(6), 2048, 4, 0), "zf": (-6, "zz", 0, "zf", 0, 256, 1, 0), "of": (-6, "ol", 0, "of", 0, 16, 1, 1),
+                "cf": (-6, "cc", 16, "cf", 0, 16, 1, 1), "yf": (-5, "yws", 0, "ywr", 0, 256, 1, 2), "nf": (-5, "nsx", 0, "nsr", 0, 32, 1, 3)}[name]
     t = int(name[1:])
-    return {"x": (1, "xb%d" % (t - 1), "xb%d" % t, 256, 2048, 4, 0), "h": (1, "hl%d" % (t - 1), "hl%d" % t, 0, NH, 4, 0),
-            "a": (1, "amo", "ami", 2 * t, 2, 1, 1)}[name[0]]
+    return {"x": (1, "XB", slot(t - 1), "XB", slot(t), XW, 4, 0), "h": (1, "tb%d" % (t - 1), 0, "tb%d" % t, 0, 1024, 4, 0),
+            "a": (1, "amo", t, "ami", t, 1, 1, 1)}[name[0]]
 
 
 def order():
-    o = ["x1", "h1", "h2"]
+    o = ["h1", "x1", "h2"]
     for t in range(1, TV):
         o.append("a%d" % t)
         o.append("x%d" % (t + 1) if t + 1 < TV else "xf")
         if t + 2 < TV:
             o.append("h%d" % (t + 2))
-    return o + ["zf", "cf", "yf", "nf"]
+    return o + ["of", "zf", "cf", "yf", "nf"]
 
 
 def route(name, src, dst, topo):
-    _, _, _, c0, w, pieces, first = message(name)
+    w, pieces, first = message(name)[5:8]
     if topo.may_write(src, dst):
-        return [(None, c0, w)]
+        return [(None, 0, w)]
     hs = [h for h in topo.cores_of(src) if topo.may_write(h, dst)]
     hs = [h for h in hs if topo.die(h) == topo.die(src)] + [h for h in hs if topo.die(h) != topo.die(src)]
     pieces = min(pieces, len(hs))
     pick = hs[first % len(hs):] + hs[:first % len(hs)]
-    return [(pick[j], c0 + w // pieces * j, w // pieces) for j in range(pieces)]
+    return [(pick[j], w // pieces * j, w // pieces) for j in range(pieces)]
 
 
 def peer(name, rank):
     return (rank - message(name)[0]) % 8
 
 
-def put(g, T, topo, core, dst, sem, out, in_):
+def put(g, T, topo, core, dst, sem, out, in_, local="L"):
     rid, pid = topo.addr(dst, core)
-    g.remote_dma(out, in_, T.sem[sem], T.sem.L, pid, rid, topo.mask(core, dst))
+    g.remote_dma(out, in_, T.sem[sem], T.sem[local], pid, rid, topo.mask(core, dst))
     return len(topo.engines(core, dst))
 
 
@@ -92,9 +96,10 @@ def helper_program(g, core, T, topo):
             way = route(name, src, dst, topo)
             for h, c0, w in way:
                 if h == core:
-                    buf = T[message(name)[2]]
+                    db, d0 = message(name)[3:5]
+                    piece = T[db][:, d0 + c0:d0 + c0 + w]
                     g.wait_ge(T.sem["r_" + name], len(topo.engines(src, core)) // len(way))
-                    sent += put(g, T, topo, core, dst, "r_" + name, buf[:, c0:c0 + w], buf[:, c0:c0 + w])
+                    sent += put(g, T, topo, core, dst, "r_" + name, piece, piece)
     if sent:
         g.wait_ge(T.sem.L, sent)
 
@@ -113,10 +118,9 @@ def rank_program(g, core, T, topo):
             Q[q].wait_ge(T.sem[sem], val)
             seen[q][sem] = val
 
-    def deps(q, R, W, B, dma):
+    def deps(q, R, W, B):
         for k in R:
-            if k in last:
-                need(q, last[k])
+            need(q, last[k])
         for k in W:
             for tok in ([last[k]] if k in last else []) + list(read.get(k, {}).values()):
                 need(q, tok)
@@ -136,39 +140,40 @@ def rank_program(g, core, T, topo):
             bank.setdefault(b, {})[q] = tok
 
     def run(q, call, R=(), W=(), B=()):
-        deps(q, R, W, B, False)
+        deps(q, R, W, B)
         cnt[q] += 1
         call().then_inc(T.sem[q], 1)
         total[q] = cnt[q]
         note(q, (q, cnt[q], q), R, W, B)
 
     def dma(q, sem, pairs, R=(), W=()):
-        deps(q, R, W, (), True)
+        deps(q, R, W, ())
         for out, in_ in pairs:
             Q[q].dma_start(out, in_).then_inc(T.sem[sem], 16)
             total[sem] = total.get(sem, 0) + 16
         note(q, (sem, total[sem], None), R, W, ())
 
-    sent = [0]
-
-    def send(name, R):
+    def send(name, R, local="L"):
         dst = T.cores[peer(name, rank)]
-        sb, db = message(name)[1:3]
-        deps("G", R, (), (), True)
+        sb, s0, db, d0 = message(name)[1:5]
+        deps("G", R, (), ())
         way = route(name, core, dst, topo)
         if len(way) == 1:
             h, c0, w = way[0]
-            sent[0] += put(g, T, topo, core, dst if h is None else h, "r_" + name, T[db][:, c0:c0 + w], T[sb][:, c0:c0 + w])
-            return
-        trs = []
-        for j, (h, c0, w) in enumerate(way):
-            es = topo.engines(core, h)
-            es = es[j * (len(es) // len(way)):(j + 1) * (len(es) // len(way))]
-            rid, pid = topo.addr(h, core)
-            trs.append(RemoteDMATransfer(dst_ids=[DstId(rid=rid, pnc=pid)], dma_engine_mask=sum(1 << e for e in es),
-                                         remote_sem=T.sem["r_" + name], srcs=[T[sb][:, c0:c0 + w]], dsts=[T[db][:, c0:c0 + w]]))
-            sent[0] += len(es)
-        g.remote_dma_fused(trs, local_sem=T.sem.L)
+            n = put(g, T, topo, core, dst if h is None else h, "r_" + name, T[db][:, d0:d0 + w], T[sb][:, s0:s0 + w], local)
+        else:
+            trs, n = [], 0
+            for j, (h, c0, w) in enumerate(way):
+                es = topo.engines(core, h)
+                es = es[j * (len(es) // len(way)):(j + 1) * (len(es) // len(way))]
+                rid, pid = topo.addr(h, core)
+                trs.append(RemoteDMATransfer(dst_ids=[DstId(rid=rid, pnc=pid)], dma_engine_mask=sum(1 << e for e in es), remote_sem=T.sem["r_" + name],
+                                             srcs=[T[sb][:, s0 + c0:s0 + c0 + w]], dsts=[T[db][:, d0 + c0:d0 + c0 + w]]))
+                n += len(es)
+            g.remote_dma_fused(trs, local_sem=T.sem[local])
+        total[local] = total.get(local, 0) + n
+        if local != "L":
+            note("G", (local, n, None), R, (), ())
 
     def landing(name, key):
         src = T.cores[(rank + message(name)[0]) % 8]
@@ -191,8 +196,11 @@ def rank_program(g, core, T, topo):
     def cp(out, in_, R=(), W=(), B=()):
         run("V", lambda: g.vector.tensor_copy(out, in_), R, W, B)
 
-    def fill(out, c, W, R=()):
-        run("V", lambda: g.vector.memset(out, c), R, W)
+    def scan(out, d0, d1, op0, op1, R=(), W=(), B=()):
+        run("V", lambda: g.vector.tensor_tensor_scan(out, d0, d1, 0.0, op0, op1), R, W, B)
+
+    def fill(out, c, W, B=()):
+        run("V", lambda: g.vector.memset(out, c), (), W, B)
 
     def act(out, in_, func=AF.Copy, R=(), W=(), B=(), **kw):
         run("S", lambda: g.scalar.activation(out, in_, func, **kw), R, W, B)
@@ -204,358 +212,348 @@ def rank_program(g, core, T, topo):
         for j, (l, r, keys) in enumerate(parts):
             mm(out, l, r, j == 0, j == len(parts) - 1, keys, (bk,))
 
-    dma("S", "i_ls", [(T.lsi[:], T.ls[:])], W=["lsi"])
+    XB, cF = T.XB, T.cF
     dma("Y", "i_ns", [(T.nsd[0:8, 0:256], T.nl[:]), (T.nsd[0:8, 256:512], T.sd[:])], W=["nsd"])
+    dma("S", "i_ls", [(T.tb0[0:112, :], T.ls[16:128, :]), (T.tb0[112:128, :], T.ls[0:16, :])], W=["tb0"])
+    dma("Y", "i_wd", [(T.wdi[0:112, :], T.wd[16:128, :]), (T.wdi[112:128, :], T.wd[0:16, :])], W=["wdi"])
+    dma("Y", "i_x", [(T.xr[:], T.x[:])], W=["xr"])
     dma("Y", "i_th", [(T.thi[0:8, :], T.th[:])], W=["thi"])
     dma("Y", "i_wt", [(T.wti[:], T.wt[:])], W=["wti"])
-    dma("Y", "i_x", [(T.xr[:], T.x[:])], W=["xr"])
-    dma("Y", "i_wd", [(T.wdi[:], T.wd[:])], W=["wdi"])
     run("G", lambda: g.iota(T.pc[:], [[0, 1]], 0, 1), (), ["pc"])
-    run("G", lambda: g.iota(T.dif[:], [[1, 128]], 256, -1), (), ["dif"])
     run("G", lambda: g.iota(T.mi[:], [[1, 144]], 0, 0), (), ["mi"])
-    run("G", lambda: g.iota(T.bi[:], [[16, 16]], 0, 0), (), ["bi"])
-    run("G", lambda: g.iota(T.TL[:, 8192:10240], [[0, 2048]], 0, 0, allow_small_or_imprecise_dtypes=True), (), ["TLc"])
-    fill(T.TL[:, 0:2048], 0.0, ["TLa"])
-    fill(T.TL[:, 2048:8192], 0.0, ["TLd"])
-    for j in range(3):
-        act(T.TL[:, 10240 + 2048 * j:12288 + 2048 * j], T.TL[:, 0:2048], R=["TLa"], W=["TLb%d" % j])
-    act(T.xb0[:, 256:NX], T.xr[:], R=["xr"], W=["xb0"], bias=128.0)
-
-    cF = T.cF
+    run("G", lambda: g.iota(T.dif[:], [[1, 128]], 256, -1), (), ["dif"])
+    run("G", lambda: g.iota(T.jj[:], [[16, 16]], 0, 0), (), ["jj"])
+    for t in range(1, TV):
+        landing("x%d" % t, "x%d" % t)
+        landing("h%d" % t, "tb%d" % t)
+        landing("a%d" % t, "am%d" % t)
+    for n, k in (("xf", "x%d" % TV), ("zf", "zf"), ("of", "of"), ("cf", "cf"), ("yf", "ywr"), ("nf", "nsr")):
+        landing(n, k)
+    send("h1", ["tb0"])
 
     def col(j):
         return cF[:, j:j + 1]
-    ts(T.cI[:, 0:1], T.pc[:], 15, None, A.bitwise_and, R=["pc"], W=["cI"])
-    ts(T.cI[:, 1:2], T.pc[:], 112, None, A.bitwise_and, R=["pc"], W=["cI1"])
-    cp(cF[:, 0:2], T.cI[:], R=["cI", "cI1"], W=["c0"])
+    fill(T.ones[:], 1.0, ["ones"])
+    fill(T.win[:, 256:1280], 0.0, ["win1"])
+    for j in range(5):
+        act(T.win[:, 1280 + 208 * j:min(2304, 1488 + 208 * j)], T.ones[:, 0:min(208, 1024 - 208 * j)], R=["ones"], W=["wz%d" % j])
+    fill(T.one32[:], 1.0, ["one32"])
+    fill(T.RM[:], 1.0, ["RM"])
+    fill(T.Z0[:], BIG, ["Z0"])
+    fill(T.CZ[:], 0.0, ["CZ"])
+    fill(T.CY[:], 0.0, ["CY"])
+    fill(T.K[:], 6656.0, ["K"])
+    fill(T.F[:], 0.0, ["F"])
+    fill(T.RM[:, 0:512:8], 0.0, ["RM"])
+    fill(T.Z0[:, 0:128:8], -BIG, ["Z0"])
+    fill(T.CZ[:, 2:128:8], -14.0 * SC, ["CZ"])
+    fill(T.CY[:, 0:128:8], 1.0, ["CY"])
+    fill(XB[:, slot(0) + NTH:slot(0) + XW], 0.0, ["par"])
+    fill(T.DX[:, 0:32:2], -2048.0, ["dw"])
+    fill(T.Z0[:, 3:128:8], -BIG, ["Z0"])
+    fill(T.CZ[:, 4:128:8], 2.0 * 2 ** TAG, ["CZ"])
+    fill(T.CY[:, 4:128:8], 3.0, ["CY"])
+    fill(T.DX[:, 128:160:2], float(XW), ["dc"])
+    fill(T.CZ[:, 144:160], 7.0 * 2 ** TAG, ["CZ"])
+    fill(T.CY[:, 128:144], -1.0, ["CY"])
+    ts(T.cI[:, 0:1], T.pc[:], 15, None, A.bitwise_and, R=["pc"], W=["i0"])
+    ts(T.cI[:, 1:2], T.pc[:], 112, None, A.bitwise_and, R=["pc"], W=["i1"])
+    ts(T.cI[:, 2:3], T.pc[:], 16.0, None, A.add, R=["pc"], W=["i2"])
+    ts(T.cI[:, 3:4], T.pc[:], 16.0, 127.0, A.mult, A.add, R=["pc"], W=["i3"])
+    fill(T.CZ[:, 6:128:8], -10.0 * SC, ["CZ"])
+    fill(T.CY[:, 144:160], 8.0, ["CY"])
+    ts(T.cI[:, 2:3], T.cI[:, 2:3], 112, None, A.bitwise_and, R=["i2"], W=["i2"])
+    ts(T.cI[:, 3:4], T.cI[:, 3:4], 127, None, A.bitwise_and, R=["i3"], W=["i3"])
+    ts(T.cI[:, 4:5], T.pc[:], 12, None, A.bitwise_and, R=["pc"], W=["i4"])
+    ts(T.cI[:, 5:6], T.pc[:], 3, None, A.bitwise_and, R=["pc"], W=["i5"])
+    cp(T.cI[:, 6:7], T.pc[:], R=["pc"], W=["i6"])
+    cp(cF[:, 0:7], T.cI[:, 0:7], R=["i%d" % j for j in range(7)], W=["c0"])
     ts(T.dif[:], T.dif[:], 127, None, A.bitwise_and, R=["dif"], W=["dif"])
-    ts(col(3), col(0), 8.0, None, A.is_lt, R=["c0"], W=["c3"])
-    ts(col(4), col(0), 8.0, None, A.is_ge, R=["c0"], W=["c4"])
+    ts(T.e8r[0:8, :], T.mi[0:8, :], cF[0:8, 3:4], None, A.is_equal, R=["mi", "c0"], W=["e8r"])
+    cp(T.src8[0:8, 0:512], T.nsd[0:8, :], R=["nsd"], W=["src8"])
+    ts(col(8), col(0), 7.0, None, A.is_lt, R=["c0"], W=["c8"])
+    ts(col(10), col(0), 15.0, None, A.is_lt, R=["c0"], W=["c10"])
+    tt(T.src8[0:8, 512:768], T.nsd[0:8, 256:512], T.src8[0:8, 256:512], A.subtract, R=["nsd", "src8"], W=["src8b"])
+    msum(T.pb7[:, 0:48], 7, [(T.e8r[0:8, 15 - a:143 - a], T.src8[0:8, a:768:16], ["e8r", "src8", "src8b"]) for a in range(16)])
+    tt(col(9), col(10), col(8), A.subtract, R=["c10", "c8"], W=["c9"])
+    ts(T.EQ[:], T.mi[:, 0:16], col(0), None, A.is_equal, R=["mi", "c0"], W=["EQ"])
 
     def mat(name, d, c):
-        ts(T[name][:], T.dif[:], float(d), col(c), A.is_equal, A.mult, R=["dif", "c%d" % c], W=[name])
-    mat("LOs", 0, 3)
-    mat("LOq", 8, 3)
-    mat("HIe", 120, 4)
-    mat("HIo", 0, 4)
-    cp(T.lsH[:], T.lsi[:], R=["lsi"], W=["lsH"])
-    tt(T.lsL[:], T.lsi[:], T.lsH[:], A.subtract, R=["lsi", "lsH"], W=["lsL"])
-    zero = ["TLa", "TLb0", "TLb1", "TLb2", "TLc", "TLd"]
-    dma("Y", "tl0", [(T.TL[a::16, 1024 * a:1024 * a + 1024], T.lsH[a::16, :]) for a in range(16)], R=zero + ["lsH"], W=["TL"])
-    for q, sem, key, a0 in (("Y", "tlb", "TLx", 0), ("S", "tlc", "TLy", 8)):
-        dma(q, sem, [(T.TL[(a + 8) % 16::16, 1024 * a:1024 * a + 1024], T.lsL[a::16, :]) for a in range(a0, a0 + 8)],
-            R=zero + ["lsL"], W=[key])
-    cp(col(12), T.pc[:], R=["pc"], W=["c12"])
-    ts(T.m4[0:8, :], T.mi[0:8, 0:128], 4, None, A.logical_shift_right, R=["mi"], W=["m4"])
-    ts(T.br[0:8, :], T.m4[0:8, :], cF[0:8, 12:13], None, A.is_equal, R=["m4", "c12"], W=["br"])
-    cp(T.thb[0:8, :], T.thi[0:8, :], R=["thi"], W=["thb"])
-    mm(T.pb6[:, 0:1], T.br[0:8, :], T.thb[0:8, :], True, True, ["br", "thb"], (6,))
-    def staging(b, l1, l2):
-        for h in range(2):
-            o = 2 * b + h
-            sl = slice(512 * h, 512 * h + 512)
-            msum(T["pb%d" % o][:, 0:512], o, [(T[l1][:], T.lsH[:, sl], [l1, "lsH"]), (T[l2][:], T.lsL[:, sl], [l2, "lsL"])])
-            act(T.hl0[:, 512 * o:512 * o + 512], T["pb%d" % o][:, 0:512], W=["hl0_%d" % o], B=(o,))
-    staging(0, "LOs", "LOq")
-    ts(col(11), T.pc[:], 16.0, 15.0, A.mult, A.add, R=["pc"], W=["c11"])
-    ts(T.e8[0:8, :], T.mi[0:8, :], cF[0:8, 11:12], None, A.is_equal, R=["mi", "c11"], W=["e8"])
-    cp(T.src8[0:8, 0:512], T.nsd[0:8, :], R=["nsd"], W=["src8"])
-    tt(T.src8[0:8, 512:768], T.nsd[0:8, 256:512], T.src8[0:8, 256:512], A.subtract, R=["nsd", "src8"], W=["src8b"])
-    msum(T.pb7[:, 0:48], 7, [(T.e8[0:8, 15 - a:143 - a], T.src8[0:8, a:768:16], ["e8", "src8", "src8b"]) for a in range(16)])
-    staging(1, "HIo", "HIe")
+        ts(T[name][:], T.dif[:], float(d), c if isinstance(c, float) else col(c), A.is_equal, A.mult,
+           R=["dif"] + ([] if isinstance(c, float) else ["c%d" % c]), W=[name])
+    ts(T.N0[:], T.mi[:, 0:128], col(2), None, A.is_equal, R=["mi", "c0"], W=["N0"])
+    ts(T.N1[:], T.mi[:, 0:128], 8.0, col(2), A.subtract, A.is_equal, R=["mi", "c0"], W=["N1"])
+    s0 = T.I[:, 32:48]
+    cp(T.s7[:], T.pb7[:, 16:32], W=["s7"], B=(7,))
+    mat("LE", 17, 8)
+    tt(s0, T.pb7[:, 32:48], T.s7[:], A.add, R=["s7"], W=["Is"], B=(7,))
+    ts(T.pre[:, 0:16], T.pb7[:, 0:16], 2464.0, None, A.mult, W=["pre"], B=(7,))
+    cp(T.nb[:], T.pb7[:, 0:16], W=["nb"], B=(7,))
+    ts(T.s32[:, 0:16], s0, 32.0, None, A.add, R=["Is"], W=["s32"])
+    ts(T.I[:, 0:16], s0, 15, None, A.bitwise_and, R=["Is"], W=["Ia"])
+    tt(T.tt[:, 0:16], T.s32[:, 0:16], s0, A.mult, R=["s32", "Is"], W=["tt"])
+    cp(T.wa[:, 16:32], T.I[:, 0:16], R=["Ia"], W=["wa"])
+    tt(T.tt[:, 0:16], T.tt[:, 0:16], T.pre[:, 0:16], A.add, R=["tt", "pre"], W=["tt"])
+    mat("LO", 25, 8)
+    ts(T.I[:, 64:80], T.tt[:, 0:16], 5, 1023, A.arith_shift_right, A.bitwise_and, R=["tt"], W=["Ic"])
+    mat("HE", 9, 9)
+    cp(T.cc[:, 0:16], T.I[:, 64:80], R=["Ic"], W=["cc"])
+    mat("HO", 17, 9)
+    cp(T.Sel[:], T.wdi[:], R=["wdi"], W=["Sel"])
+    mat("MW", 17, 10)
+    mat("roll", 16, 1.0)
+    cp(T.L[:, 65:96:2], s0, R=["Is"], W=["Ls"])
+    mat("eye", 0, 1.0)
+    mat("neg", 0, -1.0)
 
-    def sfill(out, c, key):
-        n = out.shape[1]
-        act(out, T.xr[:, 0:n], R=["xr"], W=[key], scale=0.0, bias=float(c))
+    def x_out():
+        o = slot(0)
+        cp(col(13), T.wti[:], R=["wti"], W=["c13"])
+        ts(col(14), col(1), 15.0, None, A.add, R=["c0"], W=["c14"])
+        ts(T.m4[:], T.mi[:, 0:128], 112, None, A.bitwise_and, R=["mi"], W=["m4"])
+        ts(T.Q8[:], T.mi[:], col(14), SC, A.is_equal, A.mult, R=["mi", "c14"], W=["Q8"])
+        ts(col(15), col(6), 16.0, None, A.mult, R=["c0"], W=["c15"])
+        cp(T.thb[0:8, :], T.thi[0:8, :], R=["thi"], W=["thb"])
+        ts(T.br[0:8, :], T.m4[0:8, :], cF[0:8, 15:16], -1.0, A.is_equal, A.mult, R=["m4", "c15"], W=["br"])
+        mm(T.pb6[:, 0:1], T.br[0:8, :], T.thb[0:8, :], True, True, ["br", "thb"], (6,))
+        ts(XB[:, o + QW1:o + WTB], T.Q8[:], col(13), 1.0 / SC, A.mult, A.mult, R=["Q8", "c13"], W=["p1"])
+        ts(XB[:, o + WTB:o + NTH], T.ones[:, 0:32], col(13), None, A.mult, R=["ones", "c13"], W=["p3"])
+        cp(XB[:, o + NTH:o + NTH + 1], T.pb6[:, 0:1], W=["par"], B=(6,))
+        ts(XB[:, o:o + 2048], T.xr[:], 128.0, None, A.add, R=["xr", "p1", "p3", "par"], W=["x0"])
+        send("x1", ["x0"], "l0")
 
-    def sfills():
-        sfill(T.RM[:], 1.0, "RM")
-        sfill(T.RM[:, 0:2048:8], 0.0, "RM")
-        sfill(T.one[:], 1.0, "one")
-        sfill(T.win[:, 1536:2048], 0.0, "win3")
-    sfill(T.CH[:], 0.0, "CH")
-    for j, (h, v) in enumerate(((1, -2.0 ** 24), (3, -2.0 ** 24 + 2.0 ** 22), (8, -2.0 ** 24 + 2.0 ** 23), (0, 0.0))):
-        sfill(T.TAGC[:, 16 * j:16 * j + 16], v, "TAGC")
-        if h:
-            sfill(T.KT[:, 16 * j:16 * j + 16], h, "KT")
-            sfill(T.CH[:, 16 * j:16 * j + 16], 2.0 * h * BIG + v, "CH")
-            sfill(T.CH[:, 64 + 16 * j:80 + 16 * j], -77.0 * h, "CH")
-    fill(T.hl0[:, 2050:NH], 0.0, ["hl0"])
-    cp(T.hl0[:, 2048:2049], T.wti[:], R=["wti"], W=["hl0w"])
-    cp(T.hl0[:, 2049:2050], T.pb6[:, 0:1], W=["hl0h"], B=(6,))
-    HL0 = ["hl0", "hl0w", "hl0h"] + ["hl0_%d" % o for o in range(4)]
-    ts(col(2), col(1), 15.0, None, A.add, R=["c0"], W=["c2"])
-    ts(col(6), col(0), 1.0, None, A.is_ge, R=["c0"], W=["c6"])
-    ts(col(7), col(0), 7.0, None, A.is_lt, R=["c0"], W=["c7"])
-    ts(col(9), col(0), 15.0, None, A.is_lt, R=["c0"], W=["c9"])
-    tt(col(5), col(6), col(3), A.mult, R=["c6", "c3"], W=["c5"])
-    tt(col(8), col(9), col(7), A.subtract, R=["c9", "c7"], W=["c8"])
+    def consts():
+        ts(T.grp[:], T.m4[:], col(1), -OFF, A.is_equal, A.mult, R=["m4", "c0"], W=["grp"])
+        mat("e8", 0, SC)
+        mat("e2048", 0, 256.0 * SC)
+        mat("roll5", 16, 5.0)
+        ts(col(17), col(5), 512.0, None, A.mult, R=["c0"], W=["c17"])
+        ts(col(18), col(0), 8.0, None, A.mult, R=["c0"], W=["c18"])
+        ts(col(16), col(4), 2.0, col(17), A.mult, A.add, R=["c0", "c17"], W=["c16"])
+        ts(T.J[:], T.jj[:], col(0), -1.0 / 256, A.add, A.mult, R=["jj", "c0"], W=["J"])
+        ts(T.J1[:], T.jj[:], col(0), 256.0, A.add, A.add, R=["jj", "c0"], W=["J1"])
+        ts(T.I8[:], T.jj[:], 8.0, col(18), A.mult, A.add, R=["jj", "c18"], W=["I8"])
+        ts(T.POS[:], T.jj[:], 2.0, col(16), A.mult, A.add, R=["jj", "c16"], W=["POS"])
+        ts(T.K[:, 1:32:2], T.J[:], -2464.0, 6656.0, A.mult, A.add, R=["J"], W=["K"])
+        mat("n2464", 0, -2464.0)
+        mat("eye32", 0, 1.0)
+        mat("n32", 0, -2464.0 / 256)
+        mat("roll32", 16, 1.0 / 256)
 
-    def places0():
-        ts(T.k2[:], T.sI[:], 15, None, A.bitwise_and, R=["sI"], W=["k2"])
-        tt(T.k1[:], T.sI[:], T.sI[:], A.mult, R=["sI"], W=["k1"])
-        ts(T.k1[:], T.k1[:], 5, None, A.logical_shift_right, R=["k1"], W=["k1"])
-        tt(T.k1[:], T.k1[:], T.sI[:], A.add, R=["k1", "sI"], W=["k1"])
-        ts(T.k3[:], T.nF[:], 77.0, None, A.mult, R=["nF"], W=["k3"])
-        tt(T.k1[:], T.k1[:], T.k3[:], A.add, R=["k1", "k3"], W=["k1"])
-        ts(T.k1[:], T.k1[:], 1023, None, A.bitwise_and, R=["k1"], W=["k1"])
-        ts(T.k2[:], T.k2[:], 1024.0, None, A.mult, R=["k2"], W=["k2"])
-        tt(T.k1[:], T.k1[:], T.k2[:], A.add, R=["k1", "k2"], W=["k1"])
-        cp(T.cl[:], T.k1[:], R=["k1"], W=["cl"])
-        cp(T.SelH[:], T.wdi[:], R=["wdi"], W=["SelH"])
-        tt(T.SelL[:], T.wdi[:], T.SelH[:], A.subtract, R=["wdi", "SelH"], W=["SelL"])
-        mat("LOe0", 1, 7)
-        mat("LOo0", 9, 7)
-        ts(T.N0[:], T.mi[:, 0:128], col(1), None, A.is_equal, R=["mi", "c0"], W=["N0"])
-        ts(T.N1[:], T.mi[:, 0:128], 8.0, col(1), A.subtract, A.is_equal, R=["mi", "c0"], W=["N1"])
-        mat("HIe0", 121, 8)
-        mat("HIo0", 1, 8)
+    def change(t, hf):
+        tt(XB[:, slot(t):slot(t) + XW + 2048].indirect(T.cc[:, 16 + 8 * hf:24 + 8 * hf]), T.oldh[:, 128 * hf:128 * hf + 128], T.zz[:, 128 * hf:128 * hf + 128],
+           A.add, R=["oldh", "zz", "cc"], W=["x%d" % t, "x%d" % (t - 1)])
 
-    def rest():
-        ts(T.eye[:], T.dif[:], 0.0, None, A.is_equal, R=["dif"], W=["eye"])
-        ts(T.neg[:], T.dif[:], 0.0, -1.0, A.is_equal, A.mult, R=["dif"], W=["neg"])
-        mat("M10", 1, 9)
-        ts(T.npb[:], T.nF[:], 1.0, 16.0, A.add, A.min, R=["nF"], W=["npb"])
-        ts(T.ebig[:], T.dif[:], 0.0, -BIG, A.is_equal, A.mult, R=["dif"], W=["ebig"])
-        ts(T.e77[:], T.dif[:], 0.0, 77.0, A.is_equal, A.mult, R=["dif"], W=["e77"])
-        ts(T.KT[:, 48:64], T.sI[:], 5.0, None, A.mult, R=["sI"], W=["KT3"])
-        ts(T.Q1[:], T.mi[:], col(2), None, A.is_equal, R=["mi", "c2"], W=["Q1"])
-
-    def last_consts():
-        ts(T.iB[:], T.bi[:], col(0), None, A.add, R=["bi", "c0"], W=["iB"])
-        ts(T.i8[:], T.iB[:], 8.0, 256.0 - 16384.0, A.mult, A.add, R=["iB"], W=["i8"])
-        ts(T.iBd[:], T.iB[:], 1.0 / 512, None, A.mult, R=["iB"], W=["iBd"])
-        ts(T.roll[:], T.dif[:], 16.0, None, A.is_equal, R=["dif"], W=["roll"])
-        ts(T.rollb[:], T.dif[:], 16.0, None, A.is_equal, R=["dif"], W=["rollb"])
-        mat("LOe", 0, 5)
-        mat("LOo", 8, 5)
-        mat("M1", 0, 6)
-        fill(T.amo[:], 0, ["amo"])
-    cp(T.nF[:], T.pb7[:, 0:16], W=["nF"], B=(7,))
-    cp(T.sI[:], T.pb7[:, 16:32], W=["sI"], B=(7,))
-    tt(T.sI[:], T.pb7[:, 32:48], T.sI[:], A.add, R=["sI"], W=["sI"], B=(7,))
-    places0()
-
-    def table(t):
-        hl = T["hl%d" % t]
-        dma("Y", "tl%d" % t, [(T.TL[p::8, 1024 * (p + 8 * j):1024 * (p + 8 * j) + 1024], hl[p::8, 1024 * j:1024 * j + 1024])
-                              for p in range(8) for j in range(2)],
-            R=["hl%d" % t], W=["TL", "TLx", "TLy"])
-    send("x1", ["xb0", "TL"])
-    send("h1", HL0)
-    for t in range(1, TV):
-        landing("x%d" % t, "xb%d" % t)
-        landing("h%d" % t, "hl%d" % t)
-        landing("a%d" % t, "am%d" % t)
-    for n, k in (("xf", "xf"), ("zf", "zf"), ("cf", "cf"), ("yf", "ywr"), ("nf", "nsr")):
-        landing(n, k)
-
-    PAIRS = ((0, 1), (0, 3), (1, 4), (2, 5))
-
-    def squares():
-        ts(T.f1[:], T.SF[:], 0.0, -8.0, A.is_lt, A.mult, R=["SF"], W=["f1"])
-
-    def lengths(where):
-        msum(T.pb2[:, 0:16], 2, [(T[where][:], T[k][:], [where, k]) for k in ("npb", "f1", "f2", "f3")])
-
+    WZ = ["win1"] + ["wz%d" % j for j in range(5)]
     for t in range(TV):
         end = t == TV - 1
-        xb, kx = T["xb%d" % t], ["xb%d" % t]
-        x = xb[:, 256:NX]
-        hl, kh = T["hl%d" % t], HL0 if t == 0 else ["hl%d" % t]
-        LE, LO_, HE, HO, MW = ("LOe0", "LOo0", "HIe0", "HIo0", "M10") if t == 0 else ("LOe", "LOo", "HIe", "HIo", "M1")
-        act(T.R[:], T.TL[:].indirect(T.cl[:]), R=["TL", "TLx", "TLy", "cl"], W=["R"])
-        if t == 0:
-            sfills()
+        o, kx = slot(t), "x%d" % t
+        x, kg = (XB[:, o:o + 2048], kx) if t else (T.xr[:], "xr")
+        up = 128.0 if t else 0.0
+        act(T.msk[:], T.EQ[:].indirect(T.wa[:, 16:32]), R=["EQ", "wa"], W=["msk"])
         if t:
-            act(T.SelH[:], T.win[:].indirect(T.wl[:]), R=["win", "win3", "wl"], W=["SelH"])
-            act(T.SelL[:], T.win[:, 256:2560].indirect(T.wl[:]), R=["win", "win3", "wl"], W=["SelL"])
-        ev, od = slice(0, 256, 2), slice(1, 256, 2)
-        msum(T.pb5[:, 0:128], 5, [(T.N0[:], T.R[:, ev], ["N0", "R"]), (T.N1[:], T.R[:, od], ["N1", "R"]),
-                                  (T[LE][:], T.SelH[:, ev], [LE, "SelH"]), (T[LO_][:], T.SelH[:, od], [LO_, "SelH"]),
-                                  (T[LE][:], T.SelL[:, ev], [LE, "SelL"]), (T[LO_][:], T.SelL[:, od], [LO_, "SelL"])])
-        msum(T.pb6[:, 0:128], 6, [(T[HE][:], T.SelH[:, ev], [HE, "SelH"]), (T[HO][:], T.SelH[:, od], [HO, "SelH"]),
-                                  (T[HE][:], T.SelL[:, ev], [HE, "SelL"]), (T[HO][:], T.SelL[:, od], [HO, "SelL"])])
-        cp(T.ll[:], T.pb5[:, 0:128], W=["ll"], B=(5,))
-        cp(T.lh[:], T.pb6[:, 0:128], W=["lh"], B=(6,))
-        if t == 0:
-            rest()
-        msum(T.pb7[:, 0:256], 7, [(T.N0[:], T.R[:], ["N0", "R"]), (T[MW][:], T.SelH[:], [MW, "SelH"]), (T[MW][:], T.SelL[:], [MW, "SelL"])])
-        if t:
-            lengths("rollb")
-            ts(T.KT[:, 48:64], T.sI[:], 5.0, None, A.mult, R=["sI"], W=["KT3"])
-        def gs(c):
-            s = slice(512 * c, 512 * c + 512)
-            tt(T.d8[:, s], x.indirect(T.lh[:, 32 * c:32 * c + 32]), T.G[:, s], A.subtract, R=kx + ["lh", "G%d" % c], W=["d8_%d" % c])
-        for c in range(4):
-            if c == 0:
-                act(T.G[:, 0:256], x.indirect(T.ll[:, 0:16]), R=kx + ["ll"], W=["Ga"])
-                act(T.G[:, 256:512], x.indirect(T.ll[:, 16:32]), R=kx + ["ll"], W=["G0"])
-            else:
-                act(T.G[:, 512 * c:512 * c + 512], x.indirect(T.ll[:, 32 * c:32 * c + 32]), R=kx + ["ll"], W=["G%d" % c])
-            if c == 0:
-                ts(T.QW[:], T.Q1[:], hl[:, 2048:2049], None, A.mult, R=["Q1"] + kh, W=["QW"])
-                tt(T.d8[:, 0:256], x.indirect(T.lh[:, 0:16]), T.G[:, 0:256], A.subtract, R=kx + ["lh", "Ga"], W=["d8_a"])
-                tt(T.d8[:, 256:512], x.indirect(T.lh[:, 16:32]), T.G[:, 256:512], A.subtract, R=kx + ["lh", "G0"], W=["d8_0"])
-            elif c < 3:
-                gs(c)
-            if c == 1:
-                act(T.whl[:, 0:256], T.pb7[:, 0:256], W=["wH"], B=(7,))
-                tt(T.whl[:, 256:512], T.pb7[:, 0:256], T.whl[:, 0:256], A.subtract, R=["wH"], W=["wL"], B=(7,))
-            for p, (i, j) in enumerate(PAIRS):
-                o = T["pb%d" % (p // 2)][:, 256 * (p % 2) + 64 * c:256 * (p % 2) + 64 * c + 64]
-                msum(o, p // 2, [(T.eye[:], T.G[:, 512 * c + i:512 * c + 512:8], ["eye", "G%d" % c]),
-                                 (T.neg[:], T.G[:, 512 * c + j:512 * c + 512:8], ["neg", "G%d" % c])])
-        w, W2 = T.win, T.whl
-        mv = []
-        for blk, h in ((0, 1), (1, 3), (2, 8), (4, 0)):
-            o = slice(512 * blk, 512 * blk + 512)
-            if end:
-                mv.append((w[0:128 - h, o], W2[h:128, :]))
-            else:
-                d = 17 - h
-                mv += [(w[d:128, o], W2[0:128 - d, :]), (w[0:d, o], W2[128 - d:128, :])]
-        dma("Y", "wi%d" % t, mv, R=["wH", "wL"], W=["win"])
-        if not end:
-            table(t + 1)
-        if t == 0:
-            g.sync.sem_inc(T.sem.q, 1)
-            total["q"] = 1
-            need("G", ("q", 1))
-            send("h2", ["hl1"])
-        if t and t + 2 < TV:
-            send("h%d" % (t + 2), ["hl%d" % (t + 1), "win"])
-
-        if t:
-            ts(T.npb[:], T.pb2[:, 0:16], 1.0, 16.0, A.add, A.min, W=["npb"], B=(2,))
-        mm(T.pb6[:, 128:256], T.eye[:], T.CH[:], True, False, ["eye", "CH"], (6,))
-        for j in range(8):
-            mm(T.pb6[:, 128 + 16 * j:144 + 16 * j], T["ebig" if j < 4 else "e77"][:], T.npb[:], False, j == 7, ["ebig", "e77", "npb"], (6,))
-        run("V", lambda: g.vector.tensor_tensor_scan(T.P[:], T.RM[:], T.G[:], 0.0, A.mult, A.max), ["RM", "G0", "G1", "G2", "G3"], ["P"])
-        tt(T.TAG[:], T.pb6[:, 128:192], T.TAGC[:], A.max, R=["TAGC"], W=["TAG"], B=(6,))
-        for s, e in enumerate((0, 2, 7, 0)):
-            ts(T.Zc[:, 256 * s:256 * s + 256], T.P[:, e:2048:8], -128.0, None, A.add, R=["P"], W=["Zc%d" % s])
-        gs(3)
-        if t == 0:
-            last_consts()
-
-        def ab(c):
-            act(T.ab8[:, 4 * c:4 * c + 4, :], T.d8[:, 512 * c:512 * c + 512], AF.Abs, R=["d8_%d" % c], W=["ab8_%d" % c])
-
-        def d8sum(hf):
-            bk = (2, 5)[hf]
-            msum(T["pb%d" % bk][:, 0:64], bk, [(T.Q1[:, 15 - a:143 - a], T.ab8[:, 8 * hf:8 * hf + 8, 8 * a:8 * a + 8],
-                                                      ["Q1", "ab8_%d" % (2 * hf), "ab8_%d" % (2 * hf + 1)]) for a in range(16)])
-        ab(0)
-        ab(1)
-        d8sum(0)
-        for p in range(4):
-            act(T.ab13[:, 256 * p:256 * p + 256], T["pb%d" % (p // 2)][:, 256 * (p % 2):256 * (p % 2) + 256], AF.Abs, W=["ab13_%d" % p], B=(p // 2,))
-        ab(2)
-        ab(3)
-        tb = T.xf if end else T["xb%d" % (t + 1)]
-        sfill(tb[:, 0:256], 128.0, "xft" if end else "xt%d" % (t + 1))
-        zpart = (T.pb4[:, 0:64], 4, [(T.QW[:, 15 - a:143 - a], T.Zc[:, a:1024:16], ["QW", "Zc0", "Zc1", "Zc2", "Zc3"]) for a in range(16)])
-        msum(zpart[0], zpart[1], zpart[2])
-        msum(T.pb3[:, 0:64], 3, [(T.Q1[:, 15 - a:143 - a], T.ab13[:, a:1024:16], ["Q1"] + ["ab13_%d" % p for p in range(4)]) for a in range(16)])
-        d8sum(1)
-
-        if t:
-            tt(T.Bc[:], hl[:, 2049:2050], T.ami[:, 2 * t:2 * t + 1], A.add, R=kh + ["am%d" % t], W=["Bc"])
+            act(T.Sel[:], T.win[:].indirect(T.wa[:, 0:16]), R=["win", "win0", "wa"] + WZ, W=["Sel"])
+            mm(T.pb3[:, 0:1], T.one32[:], T.cnt[:], True, True, ["one32", "cnt"], (3,))
+            msum(T.pb4[:, 128:144], 4, [(T.roll[:], T.r15[:], ["roll", "r15"]), (T.eye[:], T.J[:], ["eye", "J"]), (T.roll32[:], T.L[:, 1:32:2], ["roll32", "La"])])
+            act(T.Fs[:], T.pb3[:, 0:1], W=["Fs"], B=(3,), bias=2048.0)
+            act(T.rr[:], T.pb3[:, 0:1], W=["rr"], B=(3,), scale=0.0625, bias=128.46875)
+            act(T.r15[:], T.pb4[:, 128:144], AF.Relu, W=["r15"], B=(4,), bias=-1.0)
+            act(T.amo[:, t:t + 1], T.rr[:], AF.Identity, R=["rr", "Fs"], W=["amo%d" % t], scale=-16.0, bias=T.Fs[:])
+            send("a%d" % t, ["amo%d" % t])
+            change(t, 0)
         else:
-            cp(T.Bc[:], hl[:, 2049:2050], R=kh, W=["Bc"])
-        tt(T.s4[:], T.pb4[:, 0:64], T.KT[:], A.add, R=["KT", "KT3"], W=["s4"], B=(4,))
-        ts(T.s4[:], T.s4[:], 4095, None, A.bitwise_and, R=["s4"], W=["s4"])
-        tt(T.sq[:], T.s4[:], T.s4[:], A.mult, R=["s4"], W=["sq"])
-        ts(T.f[:], T.s4[:], 1024.0, None, A.mult, R=["s4"], W=["f"])
-        ts(T.sq[:], T.sq[:], 5, None, A.logical_shift_right, R=["sq"], W=["sq"])
-        tt(T.u[:], T.s4[:], T.pb6[:, 192:256], A.add, R=["s4"], W=["u"], B=(6,))
-        tt(T.cand[:], T.TAG[:], T.f[:], A.add, R=["TAG", "f"], W=["cand"])
-        tt(T.u[:], T.u[:], T.sq[:], A.add, R=["u", "sq"], W=["u"])
-        run("V", lambda: g.vector.tensor_tensor_scan(T.M8[:, 0:64], T.RM[:, 0:64], T.pb2[:, 0:64], 0.0, A.mult, A.max), ["RM"], ["M8"], (2,))
-        ts(T.u[:], T.u[:], 1023, None, A.bitwise_and, R=["u"], W=["u"])
-        ts(T.c13[:], T.pb3[:, 0:64], T.Bc[:], BIG, A.is_gt, A.mult, R=["Bc"], W=["c13"], B=(3,))
-        tt(T.cand[:], T.cand[:], T.u[:], A.add, R=["cand", "u"], W=["cand"])
-        tt(T.c13[:, 16:32], T.c13[:, 16:32], T.c13[:, 32:48], A.max, R=["c13"], W=["c13"])
-        tt(T.c13[:, 16:32], T.c13[:, 16:32], T.c13[:, 48:64], A.max, R=["c13"], W=["c13"])
-        run("V", lambda: g.vector.tensor_tensor_scan(T.M8[:, 64:128], T.RM[:, 0:64], T.pb5[:, 0:64], 0.0, A.mult, A.max), ["RM"], ["M8b"], (5,))
-        tt(T.e13[:], T.c13[:, 0:32], T.cand[:, 0:32], A.add, R=["c13", "cand"], W=["e13"])
-        ts(T.c8[:], T.M8[:, 7:128:8], T.Bc[:], BIG, A.is_gt, A.mult, R=["M8", "M8b", "Bc"], W=["c8"])
-        tt(T.E[:], T.e13[:, 0:16], T.e13[:, 16:32], A.min, R=["e13"], W=["E"])
-        tt(T.c8[:], T.c8[:], T.cand[:, 32:48], A.add, R=["c8", "cand"], W=["c8"])
-        tt(T.E[:], T.E[:], T.cand[:, 48:64], A.min, R=["E", "cand"], W=["E"])
-        tt(T.SI[:], T.c8[:], T.E[:], A.min, R=["c8", "E"], W=["SI"])
-        tt(T.SF[:], T.c8[:], T.E[:], A.min, R=["c8", "E"], W=["SF"])
-        ts(T.k1[:], T.SI[:], 14, 768, A.arith_shift_right, A.bitwise_and, R=["SI"], W=["k1"])
-        ts(T.k2[:], T.SI[:], 10, 7 + 16384, A.arith_shift_right, A.bitwise_and, R=["SI"], W=["k2"])
-        tt(T.k1[:], T.k1[:], T.iB[:], A.add, R=["k1", "iB"], W=["k1"])
-        tt(T.k2[:], T.k2[:], T.i8[:], A.add, R=["k2", "i8"], W=["k2"])
-        cp(T.zl[:], T.k1[:], R=["k1"], W=["zl"])
-        act(T.zz[:], T.Zc[:].indirect(T.zl[:]), R=["Zc0", "Zc1", "Zc2", "Zc3", "zl"], W=["zz"], scale=0.5, bias=31.75)
+            mm(T.pb4[:, 128:144], T.roll[:], T.nb[:], True, True, ["roll", "nb"], (4,))
+            act(T.r15[:], T.pb4[:, 128:144], AF.Relu, W=["r15"], B=(4,), scale=-1.0, bias=15.0)
+        tt(T.R[:], T["tb%d" % t][:].indirect(T.cc[:, 0:16]), T.msk[:], A.mult, R=["tb%d" % t, "cc", "msk"], W=["R"])
+        if t:
+            change(t, 1)
+            send("x%d" % (t + 1) if not end else "xf", [kx], "l%d" % t)
+        for half in (1, 0):
+            for c in range(4):
+                ev, od = slice(c, 256, 8), slice(c + 4, 256, 8)
+                out = T["pb5" if c == 0 else "pb6"][:, 64 * c + 32 * half:64 * c + 32 * half + 32]
+                E, O = ("HE", "HO") if half else ("LE", "LO")
+                msum(out, 5 if c == 0 else 6, [(T[E][:], T.Sel[:, ev], [E, "Sel"]), (T[O][:], T.Sel[:, od], [O, "Sel"])]
+                     + ([] if half else [(T.N0[:], T.R[:, ev], ["N0", "R"]), (T.N1[:], T.R[:, od], ["N1", "R"])]))
+        cp(T.ll[:, 0:64], T.pb5[:, 0:64], W=["ll0"], B=(5,))
+        cp(T.ll[:, 64:256], T.pb6[:, 64:256], W=["ll1"], B=(6,))
+        msum(T.pb7[:, 0:256], 7, [(T.MW[:], T.Sel[:], ["MW", "Sel"]), (T.N0[:], T.R[:], ["N0", "R"])])
+
+        def kl(c):
+            return "ll0" if c == 0 else "ll1"
+
+        def gather(c, w0=0, w1=64, key=None):
+            act(T.G[:, 512 * c + 8 * w0:512 * c + 8 * w1], x.indirect(T.ll[:, 64 * c + w0 // 2:64 * c + w1 // 2]), R=[kg, kl(c)], W=[key or "G%d" % c], bias=OFF - up)
+
+        def d8(c, w0=0, w1=64, key=None, out=None):
+            tt(T.d8[:, 512 * c + 8 * w0:512 * c + 8 * w1], x.indirect(T.ll[:, 64 * c + 32 + w0 // 2:64 * c + 32 + w1 // 2]),
+               T.G[:, 512 * c + 8 * w0:512 * c + 8 * w1], A.subtract, R=[kg, kl(c), key or "G%d" % c], W=[out or "d8_%d" % c])
+
+        def most(c):
+            scan(T.P[:, 512 * c:512 * c + 512], T.RM[:], T.G[:, 512 * c:512 * c + 512], A.mult, A.max, R=["RM", "G%d" % c], W=["P%d" % c])
+
+        def diffs(c):
+            for p, (i, j) in enumerate(((0, 1), (0, 3), (1, 4), (2, 5))):
+                msum(T["pb%d" % (c % 2)][:, 256 * (c // 2) + p:256 * (c // 2) + 256:4], c % 2,
+                     [(T.eye[:], T.G[:, 512 * c + i:512 * c + 512:8], ["eye", "G%d" % c]), (T.neg[:], T.G[:, 512 * c + j:512 * c + 512:8], ["neg", "G%d" % c])])
+
+        def ab13(c):
+            act(T.ab13[:, 16 * c:16 * c + 16, :], T["pb%d" % (c % 2)][:, 256 * (c // 2):256 * (c // 2) + 256], AF.Abs, W=["ab13_%d" % c], B=(c % 2,))
+
+        def ab8(c):
+            act(T.ab8[:, 16 * c:16 * c + 16, :], T.d8[:, 512 * c:512 * c + 512], AF.Abs, R=["d8_%d" % c], W=["ab8_%d" % c], bias=OFF - up)
+
+        def sum13(c):
+            for b in range(4):
+                a = c + 4 * b
+                mm(T.pb2[:, 1:128:2], T.Q8[:, 15 - a:143 - a], T.ab13[:, 16 * c:16 * c + 16, 4 * b:4 * b + 4], False, a == 15, ["Q8", "ab13_%d" % c], (2,))
+
+        def sum8(c):
+            for b in range(4):
+                a = c + 4 * b
+                mm(T.pb4[:, 0:128], T.Q8[:, 15 - a:143 - a], T.ab8[:, 16 * c:16 * c + 16, 8 * b:8 * b + 8], False, a == 15, ["Q8", "ab8_%d" % c], (4,))
+
+        def sum0(c):
+            for b in range(4):
+                a = c + 4 * b
+                for j, e in ((slice(0, 128, 8), 0), (slice(4, 128, 8), 2), (slice(144, 160), 7)):
+                    mm(T.pb2[:, j], XB[:, o + QW1 + 15 - a:o + QW1 + 143 - a], T.P[:, 512 * c + 8 * b + e:512 * c + 512:32], False, False, [kx, "P%d" % c], (2,))
+
+        def limit():
+            nth = XB[:, o + NTH:o + NTH + 1]
+            if t:
+                act(T.Bt[:], T.ones[:, 0:128], AF.Identity, R=["ones", kx, "am%d" % t], W=["Bt"], scale=T.ami[:, t:t + 1], bias=nth)
+            else:
+                act(T.Bt[:], T.ones[:, 0:128], AF.Identity, R=["ones", kx], W=["Bt"], scale=0.0, bias=nth)
+
+        gather(0, 0, 32, "Ga")
+        gather(0, 32, 64)
+        if t == 0:
+            x_out()
+        cp(T.win[:, 0:256], T.pb7[:, 0:256], W=["win0"], B=(7,))
+        d8(0, 0, 32, "Ga", "d8_a")
+        d8(0, 32, 64)
+        dma("Y", "wi%d" % t, [(T.win[0:128 - h, 256 * h:256 * h + 256], T.win[h:128, 0:256]) for h in (1, 3, 8)], R=["win0"] + WZ, W=["win"])
+        if t + 2 < TV:
+            send("h%d" % (t + 2), ["tb%d" % (t + 1), "win0"])
+        if t == 0:
+            consts()
+        diffs(0)
+        mm(T.pb2[:, 0:160], T.eye[:], T.CZ[:], True, False, ["eye", "CZ"], (2,))
+        mm(T.pb2[:, 0:160], T.eye[:], T.CY[:], False, False, ["eye", "CY"], (2,))
+        mm(T.pb2[:, 0:128:4], T.grp[:], XB[:, o + WTB:o + NTH], False, False, ["grp", kx], (2,))
+        mm(T.pb2[:, 144:160], T.grp[:], XB[:, o + WTB:o + WTB + 16], False, False, ["grp", kx], (2,))
+        mm(T.pb2[:, 128:144], T.roll5[:], T.L[:, 65:96:2], False, False, ["roll5", "Ls"], (2,))
+        for j in (2, 6):
+            mm(T.pb2[:, j:128:8], T.e8[:], T.r15[:], False, False, ["e8", "r15"], (2,))
         if not end:
-            mm(T.pb4[:, 0:16], T.roll[:], T.SF[:], True, True, ["roll", "SF"], (4,))
+            mm(T.pb5[:, 64:96], T.eye32[:], T.K[:], True, False, ["eye32", "K"], (5,))
+            for j in (0, 1):
+                mm(T.pb5[:, 64 + j:96:2], T.n2464[:], T.r15[:], False, False, ["n2464", "r15"], (5,))
+        most(0)
+        gather(1)
+        diffs(1)
+        sum0(0)
+        d8(1)
+        most(1)
+        gather(2)
+        ab13(0)
+        diffs(2)
+        sum0(1)
+        sum13(0)
+        most(2)
+        d8(2)
+        gather(3)
+        most(3)
+        ab13(1)
+        sum0(2)
+        diffs(3)
+        sum13(1)
+        sum0(3)
+        limit()
+        ab13(2)
+        sum13(2)
+        mm(T.pb2[:, 1:128:2], T.e8[:], T.Bt[:, 0:64], False, False, ["e8", "Bt"], (2,))
+        ab13(3)
+        sum13(3)
+        mm(T.pb4[:, 0:128], T.e8[:], T.Bt[:], True, False, ["e8", "Bt"], (4,))
+        mm(T.pb4[:, 0:128:8], T.e2048[:], T.r15[:], False, False, ["e2048", "r15"], (4,))
+        d8(3, 0, 32, None, "d8_b")
+        ab8(0)
+        sum8(0)
+        n = t + 1
+        scan(T.MZ[:], T.Z0[:], T.pb2[:, 0:128], A.min, A.max, R=["Z0"], W=["MZ"], B=(2,))
+        tt(T.M13[:], T.MZ[:, 2:128:8], T.MZ[:, 7:128:8], A.min, R=["MZ"], W=["M13"])
+        tt(T.pre[:, 0:32:2], T.pb2[:, 128:144], T.MZ[:, 0:128:8], A.add, R=["MZ"], W=["pre0"], B=(2,))
+        tt(T.pre[:, 1:32:2], T.pb2[:, 144:160], T.M13[:], A.min, R=["M13"], W=["pre"], B=(2,))
+        d8(3, 32, 64)
+        ts(T.hw[:], T.pre[:, 1:32:2], TAG - 8, 7 * 256, A.arith_shift_right, A.bitwise_and, R=["pre"], W=["hw"])
+        ts(T.hm[:], T.pre[:, 1:32:2], TAG, None, A.arith_shift_right, R=["pre"], W=["hm"])
+        ts(T.I[:, 32:64], T.pre[:], 4095, None, A.bitwise_and, R=["pre", "pre0"], W=["Is"])
+        tt(T.DX[:, 1:32:2], T.hw[:], T.J1[:], A.add, R=["hw", "J1"], W=["Dh"])
+        ts(T.s7[:], T.pre[:, 1:32:2], 7, None, A.bitwise_and, R=["pre"], W=["s7"])
+        tt(T.zF[:], T.hm[:], T.POS[:], A.add, R=["hm", "POS"], W=["zF"])
+        if not end:
+            mm(T.pb5[:, 65:96:2], T.n32[:], T.DX[:, 1:32:2], False, True, ["n32", "Dh"], (5,))
+            ts(T.s32[:], T.I[:, 32:64], 32.0, None, A.add, R=["Is"], W=["s32"])
+        tt(T.DX[:, 129:160:2], T.s7[:], T.I8[:], A.add, R=["s7", "I8"], W=["Dc"])
+        cp(T.zl[:], T.zF[:], R=["zF"], W=["zl"])
+        if not end:
+            tt(T.tt[:], T.s32[:], T.I[:, 32:64], A.mult, R=["s32", "Is"], W=["tt"])
+        cp(T.ol[:], T.DX[:, 129:160:2], R=["Dc"], W=["ol"])
+        ts(T.f13[:], T.hm[:], 7.0, None, A.is_ge, R=["hm"], W=["f13"])
+        if not end:
+            tt(T.tt[:], T.pb5[:, 64:96], T.tt[:], A.add, R=["tt"], W=["tt"], B=(5,))
+            ts(T.I[:, 0:32], T.pre[:], 15, None, A.bitwise_and, R=["pre"], W=["Ia"])
+            ts(T.I[:, 64:96], T.tt[:], 5, 1023, A.arith_shift_right, A.bitwise_and, R=["tt"], W=["Ic"])
+        tt(T.DX[:, 32:128:2], T.I[:, 0:96:2], T.I[:, 1:96:2], A.subtract, R=["Is", "Ia", "Ic"], W=["Dd"])
+        cp(T.DX[:, 33:128:2], T.I[:, 1:96:2], R=["Is", "Ia", "Ic"], W=["Dx"])
         if end:
-            squares()
-            tt(T.k2[:], T.k2[:], T.iB[:], A.max, R=["k2", "iB"], W=["k2"])
-            cp(T.col[:], T.k2[:], R=["k2"], W=["col"])
-        else:
-            cp(T.SrI[:], T.pb4[:, 0:16], W=["SrI"], B=(4,))
-            ts(T.k3[:], T.SrI[:], 16383, None, A.bitwise_and, R=["SrI"], W=["k3"])
-            ts(T.sq[:, 0:16], T.SrI[:], 22, None, A.arith_shift_right, R=["SrI"], W=["sq"])
-            cp(T.cl[:], T.k3[:], R=["k3"], W=["cl"])
-            tt(T.kf[:], T.sq[:, 0:16], T.iBd[:], A.add, R=["sq", "iBd"], W=["kf"])
-            tt(T.k2[:], T.k2[:], T.iB[:], A.max, R=["k2", "iB"], W=["k2"])
-            ts(T.wl[:], T.kf[:], 512.0, 2048.0, A.mult, A.add, R=["kf"], W=["wl"])
-            cp(T.col[:], T.k2[:], R=["k2"], W=["col"])
-            squares()
-            mm(T.pb3[:, 0:16], T.one[:], T.f1[:], True, True, ["one", "f1"], (3,))
-            n = t + 1
-            xn = T["xb%d" % n]
-            ts(T.oldh[:], xn[:].indirect(T.col[:]), 0.5, 32.0, A.mult, A.add, R=["xb%d" % n, "xt%d" % n, "col"], W=["oldh"])
-            tt(xn[:].indirect(T.col[:]), T.oldh[:], T.zz[:], A.add, R=["oldh", "zz", "col"], W=["xb%d" % n])
-            run("V", lambda: g.vector.tensor_reduce(cF[:, 13:14], T.pb3[:, 0:16], AxisListType.X, A.add), (), ["asum"], (3,))
-            ts(T.f2[:], T.SF[:], -2.0 ** 23, 5.0, A.is_lt, A.mult, R=["SF"], W=["f2"])
-            ts(T.f3[:], T.SF[:], -3.0 * 2.0 ** 22, 2.0, A.is_lt, A.mult, R=["SF"], W=["f3"])
-            ts(T.aI[:], cF[:, 13:14], -0.125, None, A.mult, R=["asum"], W=["aI"])
-            ts(T.sI[:], T.SrI[:], 10, 4095, A.arith_shift_right, A.bitwise_and, R=["SrI"], W=["sI"])
-            ts(T.amo[:, 2 * n:2 * n + 1], T.aI[:], 15, None, A.bitwise_and, R=["aI", "amo"], W=["amo%d" % n])
-            send("a%d" % n, ["amo", "amo%d" % n])
-            send("x%d" % (n + 1) if n + 1 < TV else "xf", ["xb%d" % n])
+            ts(T.zz[:], T.P[:].indirect(T.zl[:]), 0.5, None, A.mult, R=["P0", "P1", "P2", "P3", "zl"], W=["zz"])
+            send("of", ["ol"])
+            send("zf", ["zz"])
+        for c in (1, 2, 3):
+            ab8(c)
+            sum8(c)
+        if not end:
+            act(T.zz[:], T.P[:].indirect(T.zl[:]), R=["P0", "P1", "P2", "P3", "zl"], W=["zz"], scale=0.5)
+            act(T.oldh[:], XB[:, slot(n):slot(n) + 2048].indirect(T.ol[:]), R=["x%d" % n, "ol"], W=["oldh"], scale=0.5, bias=56.0)
+        scan(T.M8[:], T.RM[:, 0:128], T.pb4[:, 0:128], A.mult, A.max, R=["RM"], W=["M8"], B=(4,))
+        for j in (0, 1):
+            tt(T.F[:, 32 * j + 1:32 * j + 32:2], T.M8[:, 7:128:8], T.f13[:], A.min, R=["M8", "f13", "F"], W=["F%d" % j])
+        pairs = [(0, "La", "wa", ["Dh", "dw"]), (96, "Lc", "cc", ["Dc", "dc"])]
+        for c0, k, _, more in pairs[::-1] if end else pairs:
+            scan(T.L[:, c0:c0 + 64], T.F[:], T.DX[:, c0:c0 + 64], A.mult, A.add, R=["F0", "F1", "Dd", "Dx"] + more, W=[k])
+        for c0, k, out, _ in pairs[::-1] if end else pairs:
+            cp(T[out][:], T.L[:, c0 + 1:c0 + 64:2], R=[k], W=[out])
+        scan(T.L[:, 64:96], T.F[:, 0:32], T.DX[:, 64:96], A.mult, A.add, R=["F0", "Dd", "Dx"], W=["Ls"])
+        if not end:
+            act(T.junk[:], T.F[:, 1:32:2], R=["F0"], W=["junk", "cnt"], accum_out=T.cnt[:])
 
-    send("zf", ["zz"])
-    send("cf", ["col"])
-    ts(T.f2[:], T.SF[:], -2.0 ** 23, 5.0, A.is_lt, A.mult, R=["SF"], W=["f2"])
-    ts(T.f3[:], T.SF[:], -3.0 * 2.0 ** 22, 2.0, A.is_lt, A.mult, R=["SF"], W=["f3"])
-    ts(T.sq[:, 0:16], T.SI[:], 22, None, A.arith_shift_right, R=["SI"], W=["sq"])
-    lengths("eye")
-    tt(T.kf[:], T.sq[:, 0:16], T.iBd[:], A.add, R=["sq", "iBd"], W=["kf"])
-    ts(T.k1[:], T.SI[:], 10, 4095, A.arith_shift_right, A.bitwise_and, R=["SI"], W=["k1"])
-    ts(T.wl[:], T.kf[:], 512.0, 2048.0, A.mult, A.add, R=["kf"], W=["wl"])
-    cp(T.cl[:], T.pb2[:, 0:16], W=["cl"], B=(2,))
-    act(T.SelH[:], T.win[:].indirect(T.wl[:]), R=["win", "win3", "wl"], W=["SelH"])
-    act(T.SelL[:], T.win[:, 256:2560].indirect(T.wl[:]), R=["win", "win3", "wl"], W=["SelL"])
+    send("cf", ["cc"])
+    act(T.hs[:], T.win[:].indirect(T.wa[:, 0:16]), R=["win", "win0", "wa"] + WZ, W=["hs"])
     ts(T.IND[:], T.mi[:, 0:32], col(0), None, A.is_gt, R=["mi", "c0"], W=["IND"])
-    cp(T.nst[:, 0:16], T.pb2[:, 0:16], W=["nst"], B=(2,))
-    cp(T.nst[:, 16:32], T.k1[:], R=["k1"], W=["nst2"])
+    ts(T.zF[:], T.L[:, 1:32:2], -1.0 / 256, 16.0, A.mult, A.add, R=["La"], W=["zF"])
+    tt(T.M13[:], T.r15[:], T.J[:], A.add, R=["r15", "J"], W=["M13"])
+    cp(T.nst[:, 16:32], T.L[:, 65:96:2], R=["Ls"], W=["nst2"])
+    tt(T.nst[:, 0:16], T.zF[:], T.M13[:], A.subtract, R=["zF", "M13"], W=["nst"])
+    cp(T.zl[:], T.nst[:, 0:16], R=["nst"], W=["zl"])
     run("V", lambda: g.vector.transpose(T.nsx[:], T.nst[:]), ["nst", "nst2"], ["nsx"])
-    tt(T.hs[:], T.SelH[:], T.SelL[:], A.add, R=["SelH", "SelL"], W=["hs"])
-    tt(T.yws[:], T.IND[:].indirect(T.cl[:]), T.hs[:], A.mult, R=["IND", "cl", "hs"], W=["yws"])
+    tt(T.yws[:], T.IND[:].indirect(T.zl[:]), T.hs[:], A.mult, R=["IND", "zl", "hs"], W=["yws"])
     send("yf", ["yws"])
     send("nf", ["nsx"])
-    ts(T.oldh[:], T.xf[:].indirect(T.cf[:]), 0.5, 32.0, A.mult, A.add, R=["xf", "xft", "cf"], W=["oldh"])
-    tt(T.xf[:].indirect(T.cf[:]), T.oldh[:], T.zf[:], A.add, R=["oldh", "zf", "cf"], W=["xf"])
-    ts(T.xo[:, 0:1280], T.xf[:, 256:1536], -128.0, None, A.add, R=["xf"], W=["xo0"])
-    act(T.xo[:, 1280:2048], T.xf[:, 1536:NX], R=["xf"], W=["xo1"], bias=-128.0)
+    ts(T.oldh[:], XB[:, 0:2048].indirect(T.of[:]), 0.5, 56.0, A.mult, A.add, R=["x%d" % TV, "of"], W=["oldh"])
+    tt(XB[:, 0:XW + 2048].indirect(T.cf[:]), T.oldh[:], T.zf[:], A.add, R=["oldh", "zf", "cf"], W=["x%d" % TV, "x%d" % (TV - 1), "xp"])
+    ts(T.xo[:, 0:1408], XB[:, 0:1408], -128.0, None, A.add, R=["x%d" % TV], W=["xo0"])
+    act(T.xo[:, 1408:2048], XB[:, 1408:2048], R=["x%d" % TV], W=["xo1"], bias=-128.0)
     ys = []
     for a in range(4):
         for b in range(2):
             for k, y in enumerate((T.yn, T.ys)):
                 ys.append((y[2 * a + b:2 * a + b + 1, :], T.nsr[32 * a + 16 * k:32 * a + 16 * k + 16, 16 * b:16 * b + 16]))
-    dma("Y", "o_x0", [(T.yx[:, 0:1280], T.xo[:, 0:1280])], R=["xo0"])
-    dma("S", "o_x1", [(T.yx[:, 1280:2048], T.xo[:, 1280:2048])], R=["xo1"])
     dma("Y", "o_w", [(T.yw[:], T.ywr[:])], R=["ywr"])
-    dma("Y", "o_ns", ys[0::2], R=["nsr"])
-    dma("S", "o_nt", ys[1::2], R=["nsr"])
+    dma("Y", "o_ns", ys, R=["nsr"])
+    dma("Y", "o_x0", [(T.yx[:, 0:1408], T.xo[:, 0:1408])], R=["xo0"])
+    dma("S", "o_x1", [(T.yx[:, 1408:2048], T.xo[:, 1408:2048])], R=["xo1"])
     for s in total:
-        need("Y", (s, total[s]))
-    g.wait_ge(T.sem.L, sent[0])
+        need("G" if s == "L" else "Y", (s, total[s]))

from concourse.bass import DstId, RemoteDMATransfer
from concourse.mybir import AluOpType as A, ActivationFunctionType as AF

TV = 6
BIG = 1.0e20
SC = 2.0 ** 20
TAG = 17
QW1, WTB, NTH, XW = 2048, 2192, 2224, 2240
OFF = 15.5
SCRATCH = {"XB": ("sbuf", [128, (TV + 1) * XW], "bfloat16")}
for _t in range(TV):
    SCRATCH["tb%d" % _t] = ("sbuf", [128, 1024], "int32")
for _m in ("eye", "neg", "e8", "e2048", "n2464", "roll", "grp"):
    SCRATCH[_m] = ("sbuf", [128, 128], "bfloat16")
for _m in ("N0", "N1", "LE", "LO", "HE", "HO", "MW"):
    SCRATCH[_m] = ("sbuf", [128, 128], "float16")
for _m in ("eye32", "n32", "roll32", "roll5", "one32"):
    SCRATCH[_m] = ("sbuf", [128, 128], "float32")
for _b in range(8):
    SCRATCH["pb%d" % _b] = ("psum", [128, 512], "float32")
for _n, _w, _d in (
        ("xr", [2048], "bfloat16"), ("xo", [2048], "bfloat16"), ("wdi", [256], "int32"), ("win", [2304], "float32"),
        ("G", [2048], "bfloat16"), ("d8", [2048], "bfloat16"), ("P", [2048], "bfloat16"), ("RM", [512], "bfloat16"),
        ("ab8", [64, 32], "bfloat16"), ("ab13", [64, 16], "bfloat16"),
        ("Sel", [256], "float16"), ("R", [256], "float16"), ("msk", [256], "bfloat16"), ("EQ", [16], "bfloat16"),
        ("ll", [256], "uint16"), ("zl", [16], "uint16"), ("ol", [16], "uint16"), ("wa", [32], "uint16"), ("cc", [32], "uint16"), ("of", [16], "uint16"), ("cf", [16], "uint16"),
        ("zz", [256], "bfloat16"), ("oldh", [256], "bfloat16"), ("zf", [256], "bfloat16"),
        ("Q8", [144], "bfloat16"), ("dif", [128], "int32"), ("mi", [144], "int32"), ("pc", [1], "int32"), ("cI", [8], "int32"), ("cF", [24], "float32"),
        ("jj", [16], "int32"), ("POS", [16], "float32"), ("CZ", [160], "bfloat16"), ("CY", [160], "bfloat16"), ("Z0", [128], "float32"),
        ("MZ", [128], "float32"), ("M13", [16], "float32"), ("zF", [16], "float32"), ("hm", [16], "int32"), ("hw", [16], "int32"), ("I8", [16], "float32"),
        ("M8", [128], "float32"), ("f13", [16], "float32"), ("F", [64], "float32"), ("DX", [160], "float32"), ("L", [160], "float32"),
        ("I", [96], "int32"), ("pre", [32], "int32"), ("s32", [32], "int32"), ("tt", [32], "int32"), ("s7", [16], "int32"),
        ("J", [16], "bfloat16"), ("J1", [16], "float32"), ("K", [32], "float32"), ("r15", [16], "bfloat16"), ("nb", [16], "bfloat16"), ("Bt", [128], "bfloat16"), ("ones", [208], "bfloat16"),
        ("junk", [16], "float32"), ("cnt", [1], "float32"), ("Fs", [1], "float32"), ("rr", [1], "bfloat16"), ("amo", [8], "float32"), ("ami", [8], "float32"),
        ("nsd", [512], "int32"), ("src8", [768], "bfloat16"), ("e8r", [144], "bfloat16"), ("br", [128], "bfloat16"),
        ("thi", [1], "int32"), ("thb", [1], "bfloat16"), ("wti", [1], "int32"), ("m4", [128], "int32"),
        ("IND", [32], "float32"), ("hs", [256], "float32"), ("yws", [256], "float32"), ("ywr", [256], "float32"),
        ("nst", [32], "float32"), ("nsx", [32], "float32"), ("nsr", [32], "float32")):
    SCRATCH[_n] = ("sbuf", [128] + _w, _d)

RING = ["x%d" % t for t in range(1, TV)] + ["h%d" % t for t in range(1, TV)] + ["a%d" % t for t in range(1, TV)]
FIN = ["xf", "zf", "of", "cf", "yf", "nf"]
SEMAPHORES = (["V", "S", "P", "G", "L"] + ["r_" + n for n in RING + FIN] + ["wi%d" % t for t in range(TV)] + ["l%d" % t for t in range(TV)]
              + ["i_" + n for n in ("x", "ls", "wd", "ns", "th", "wt")] + ["o_" + n for n in ("x0", "x1", "w", "ns", "nt")])


def slot(t):
    return (TV - t) * XW


def message(name):
    if name in FIN:
        return {"xf": (-5, "XB", slot(5), "XB", slot(6), 2048, 4, 0), "zf": (-6, "zz", 0, "zf", 0, 256, 1, 0), "of": (-6, "ol", 0, "of", 0, 16, 1, 1),
                "cf": (-6, "cc", 16, "cf", 0, 16, 1, 1), "yf": (-5, "yws", 0, "ywr", 0, 256, 1, 2), "nf": (-5, "nsx", 0, "nsr", 0, 32, 1, 3)}[name]
    t = int(name[1:])
    return {"x": (1, "XB", slot(t - 1), "XB", slot(t), XW, 4, 0), "h": (1, "tb%d" % (t - 1), 0, "tb%d" % t, 0, 1024, 4, 0),
            "a": (1, "amo", t, "ami", t, 1, 1, 1)}[name[0]]


def order():
    o = ["h1", "x1", "h2"]
    for t in range(1, TV):
        o.append("a%d" % t)
        o.append("x%d" % (t + 1) if t + 1 < TV else "xf")
        if t + 2 < TV:
            o.append("h%d" % (t + 2))
    return o + ["of", "zf", "cf", "yf", "nf"]


def route(name, src, dst, topo):
    w, pieces, first = message(name)[5:8]
    if topo.may_write(src, dst):
        return [(None, 0, w)]
    hs = [h for h in topo.cores_of(src) if topo.may_write(h, dst)]
    hs = [h for h in hs if topo.die(h) == topo.die(src)] + [h for h in hs if topo.die(h) != topo.die(src)]
    pieces = min(pieces, len(hs))
    pick = hs[first % len(hs):] + hs[:first % len(hs)]
    return [(pick[j], w // pieces * j, w // pieces) for j in range(pieces)]


def peer(name, rank):
    return (rank - message(name)[0]) % 8


def put(g, T, topo, core, dst, sem, out, in_, local="L"):
    rid, pid = topo.addr(dst, core)
    g.remote_dma(out, in_, T.sem[sem], T.sem[local], pid, rid, topo.mask(core, dst))
    return len(topo.engines(core, dst))


def helper_program(g, core, T, topo):
    sent = 0
    for name in order():
        for r in range(8):
            src, dst = T.cores[r], T.cores[peer(name, r)]
            way = route(name, src, dst, topo)
            for h, c0, w in way:
                if h == core:
                    db, d0 = message(name)[3:5]
                    piece = T[db][:, d0 + c0:d0 + c0 + w]
                    g.wait_ge(T.sem["r_" + name], len(topo.engines(src, core)) // len(way))
                    sent += put(g, T, topo, core, dst, "r_" + name, piece, piece)
    if sent:
        g.wait_ge(T.sem.L, sent)


def rank_program(g, core, T, topo):
    rank = T.rank_of(core)
    if rank is None:
        return helper_program(g, core, T, topo)
    Q = {"V": g.vector, "S": g.scalar, "P": g.tensor, "G": g, "Y": g.sync}
    cnt, seen, last, read, bank = {q: 0 for q in Q}, {q: {} for q in Q}, {}, {}, {}
    total = {}

    def need(q, tok):
        sem, val = tok[0], tok[1]
        if seen[q].get(sem, 0) < val:
            Q[q].wait_ge(T.sem[sem], val)
            seen[q][sem] = val

    def deps(q, R, W, B):
        for k in R:
            need(q, last[k])
        for k in W:
            for tok in ([last[k]] if k in last else []) + list(read.get(k, {}).values()):
                need(q, tok)
        for b in B:
            for q2, tok in bank.get(b, {}).items():
                if q2 != q:
                    need(q, tok)

    def note(q, tok, R, W, B):
        for k in W:
            last[k] = tok
            read[k] = {}
        for k in R:
            if k not in W:
                read.setdefault(k, {})[(tok[2], tok[0])] = tok
        for b in B:
            bank.setdefault(b, {})[q] = tok

    def run(q, call, R=(), W=(), B=()):
        deps(q, R, W, B)
        cnt[q] += 1
        call().then_inc(T.sem[q], 1)
        total[q] = cnt[q]
        note(q, (q, cnt[q], q), R, W, B)

    def dma(q, sem, pairs, R=(), W=()):
        deps(q, R, W, ())
        for out, in_ in pairs:
            Q[q].dma_start(out, in_).then_inc(T.sem[sem], 16)
            total[sem] = total.get(sem, 0) + 16
        note(q, (sem, total[sem], None), R, W, ())

    def send(name, R, local="L"):
        dst = T.cores[peer(name, rank)]
        sb, s0, db, d0 = message(name)[1:5]
        deps("G", R, (), ())
        way = route(name, core, dst, topo)
        if len(way) == 1:
            h, c0, w = way[0]
            n = put(g, T, topo, core, dst if h is None else h, "r_" + name, T[db][:, d0:d0 + w], T[sb][:, s0:s0 + w], local)
        else:
            trs, n = [], 0
            for j, (h, c0, w) in enumerate(way):
                es = topo.engines(core, h)
                es = es[j * (len(es) // len(way)):(j + 1) * (len(es) // len(way))]
                rid, pid = topo.addr(h, core)
                trs.append(RemoteDMATransfer(dst_ids=[DstId(rid=rid, pnc=pid)], dma_engine_mask=sum(1 << e for e in es), remote_sem=T.sem["r_" + name],
                                             srcs=[T[sb][:, s0 + c0:s0 + c0 + w]], dsts=[T[db][:, d0 + c0:d0 + c0 + w]]))
                n += len(es)
            g.remote_dma_fused(trs, local_sem=T.sem[local])
        total[local] = total.get(local, 0) + n
        if local != "L":
            note("G", (local, n, None), R, (), ())

    def landing(name, key):
        src = T.cores[(rank + message(name)[0]) % 8]
        n = 0
        for h, _, _ in route(name, src, core, topo):
            n += len(topo.engines(src if h is None else h, core))
        last[key] = ("r_" + name, n, None)
        read[key] = {}
        total["r_" + name] = n

    def ts(out, in0, s1, s2, op0, op1=None, R=(), W=(), B=()):
        if op1 is None:
            run("V", lambda: g.vector.tensor_scalar(out, in0, s1, None, op0), R, W, B)
        else:
            run("V", lambda: g.vector.tensor_scalar(out, in0, s1, s2, op0, op1), R, W, B)

    def tt(out, a, b, op, R=(), W=(), B=()):
        run("V", lambda: g.vector.tensor_tensor(out, a, b, op), R, W, B)

    def cp(out, in_, R=(), W=(), B=()):
        run("V", lambda: g.vector.tensor_copy(out, in_), R, W, B)

    def scan(out, d0, d1, op0, op1, R=(), W=(), B=()):
        run("V", lambda: g.vector.tensor_tensor_scan(out, d0, d1, 0.0, op0, op1), R, W, B)

    def fill(out, c, W, B=()):
        run("V", lambda: g.vector.memset(out, c), (), W, B)

    def act(out, in_, func=AF.Copy, R=(), W=(), B=(), **kw):
        run("S", lambda: g.scalar.activation(out, in_, func, **kw), R, W, B)

    def mm(out, l, r, start, stop, R=(), B=()):
        run("P", lambda: g.tensor.matmul(out, l, r, start, stop), R, (), B)

    def msum(out, bk, parts):
        for j, (l, r, keys) in enumerate(parts):
            mm(out, l, r, j == 0, j == len(parts) - 1, keys, (bk,))

    XB, cF = T.XB, T.cF
    dma("Y", "i_ns", [(T.nsd[0:8, 0:256], T.nl[:]), (T.nsd[0:8, 256:512], T.sd[:])], W=["nsd"])
    dma("S", "i_ls", [(T.tb0[0:112, :], T.ls[16:128, :]), (T.tb0[112:128, :], T.ls[0:16, :])], W=["tb0"])
    dma("Y", "i_wd", [(T.wdi[0:112, :], T.wd[16:128, :]), (T.wdi[112:128, :], T.wd[0:16, :])], W=["wdi"])
    dma("Y", "i_x", [(T.xr[:], T.x[:])], W=["xr"])
    dma("Y", "i_th", [(T.thi[0:8, :], T.th[:])], W=["thi"])
    dma("Y", "i_wt", [(T.wti[:], T.wt[:])], W=["wti"])
    run("G", lambda: g.iota(T.pc[:], [[0, 1]], 0, 1), (), ["pc"])
    run("G", lambda: g.iota(T.mi[:], [[1, 144]], 0, 0), (), ["mi"])
    run("G", lambda: g.iota(T.dif[:], [[1, 128]], 256, -1), (), ["dif"])
    run("G", lambda: g.iota(T.jj[:], [[16, 16]], 0, 0), (), ["jj"])
    for t in range(1, TV):
        landing("x%d" % t, "x%d" % t)
        landing("h%d" % t, "tb%d" % t)
        landing("a%d" % t, "am%d" % t)
    for n, k in (("xf", "x%d" % TV), ("zf", "zf"), ("of", "of"), ("cf", "cf"), ("yf", "ywr"), ("nf", "nsr")):
        landing(n, k)
    send("h1", ["tb0"])

    def col(j):
        return cF[:, j:j + 1]
    fill(T.ones[:], 1.0, ["ones"])
    fill(T.win[:, 256:1280], 0.0, ["win1"])
    for j in range(5):
        act(T.win[:, 1280 + 208 * j:min(2304, 1488 + 208 * j)], T.ones[:, 0:min(208, 1024 - 208 * j)], R=["ones"], W=["wz%d" % j])
    fill(T.one32[:], 1.0, ["one32"])
    fill(T.RM[:], 1.0, ["RM"])
    fill(T.Z0[:], BIG, ["Z0"])
    fill(T.CZ[:], 0.0, ["CZ"])
    fill(T.CY[:], 0.0, ["CY"])
    fill(T.K[:], 6656.0, ["K"])
    fill(T.F[:], 0.0, ["F"])
    fill(T.RM[:, 0:512:8], 0.0, ["RM"])
    fill(T.Z0[:, 0:128:8], -BIG, ["Z0"])
    fill(T.CZ[:, 2:128:8], -14.0 * SC, ["CZ"])
    fill(T.CY[:, 0:128:8], 1.0, ["CY"])
    fill(XB[:, slot(0) + NTH:slot(0) + XW], 0.0, ["par"])
    fill(T.DX[:, 0:32:2], -2048.0, ["dw"])
    fill(T.Z0[:, 3:128:8], -BIG, ["Z0"])
    fill(T.CZ[:, 4:128:8], 2.0 * 2 ** TAG, ["CZ"])
    fill(T.CY[:, 4:128:8], 3.0, ["CY"])
    fill(T.DX[:, 128:160:2], float(XW), ["dc"])
    fill(T.CZ[:, 144:160], 7.0 * 2 ** TAG, ["CZ"])
    fill(T.CY[:, 128:144], -1.0, ["CY"])
    ts(T.cI[:, 0:1], T.pc[:], 15, None, A.bitwise_and, R=["pc"], W=["i0"])
    ts(T.cI[:, 1:2], T.pc[:], 112, None, A.bitwise_and, R=["pc"], W=["i1"])
    ts(T.cI[:, 2:3], T.pc[:], 16.0, None, A.add, R=["pc"], W=["i2"])
    ts(T.cI[:, 3:4], T.pc[:], 16.0, 127.0, A.mult, A.add, R=["pc"], W=["i3"])
    fill(T.CZ[:, 6:128:8], -10.0 * SC, ["CZ"])
    fill(T.CY[:, 144:160], 8.0, ["CY"])
    ts(T.cI[:, 2:3], T.cI[:, 2:3], 112, None, A.bitwise_and, R=["i2"], W=["i2"])
    ts(T.cI[:, 3:4], T.cI[:, 3:4], 127, None, A.bitwise_and, R=["i3"], W=["i3"])
    ts(T.cI[:, 4:5], T.pc[:], 12, None, A.bitwise_and, R=["pc"], W=["i4"])
    ts(T.cI[:, 5:6], T.pc[:], 3, None, A.bitwise_and, R=["pc"], W=["i5"])
    cp(T.cI[:, 6:7], T.pc[:], R=["pc"], W=["i6"])
    cp(cF[:, 0:7], T.cI[:, 0:7], R=["i%d" % j for j in range(7)], W=["c0"])
    ts(T.dif[:], T.dif[:], 127, None, A.bitwise_and, R=["dif"], W=["dif"])
    ts(T.e8r[0:8, :], T.mi[0:8, :], cF[0:8, 3:4], None, A.is_equal, R=["mi", "c0"], W=["e8r"])
    cp(T.src8[0:8, 0:512], T.nsd[0:8, :], R=["nsd"], W=["src8"])
    ts(col(8), col(0), 7.0, None, A.is_lt, R=["c0"], W=["c8"])
    ts(col(10), col(0), 15.0, None, A.is_lt, R=["c0"], W=["c10"])
    tt(T.src8[0:8, 512:768], T.nsd[0:8, 256:512], T.src8[0:8, 256:512], A.subtract, R=["nsd", "src8"], W=["src8b"])
    msum(T.pb7[:, 0:48], 7, [(T.e8r[0:8, 15 - a:143 - a], T.src8[0:8, a:768:16], ["e8r", "src8", "src8b"]) for a in range(16)])
    tt(col(9), col(10), col(8), A.subtract, R=["c10", "c8"], W=["c9"])
    ts(T.EQ[:], T.mi[:, 0:16], col(0), None, A.is_equal, R=["mi", "c0"], W=["EQ"])

    def mat(name, d, c):
        ts(T[name][:], T.dif[:], float(d), c if isinstance(c, float) else col(c), A.is_equal, A.mult,
           R=["dif"] + ([] if isinstance(c, float) else ["c%d" % c]), W=[name])
    ts(T.N0[:], T.mi[:, 0:128], col(2), None, A.is_equal, R=["mi", "c0"], W=["N0"])
    ts(T.N1[:], T.mi[:, 0:128], 8.0, col(2), A.subtract, A.is_equal, R=["mi", "c0"], W=["N1"])
    s0 = T.I[:, 32:48]
    cp(T.s7[:], T.pb7[:, 16:32], W=["s7"], B=(7,))
    mat("LE", 17, 8)
    tt(s0, T.pb7[:, 32:48], T.s7[:], A.add, R=["s7"], W=["Is"], B=(7,))
    ts(T.pre[:, 0:16], T.pb7[:, 0:16], 2464.0, None, A.mult, W=["pre"], B=(7,))
    cp(T.nb[:], T.pb7[:, 0:16], W=["nb"], B=(7,))
    ts(T.s32[:, 0:16], s0, 32.0, None, A.add, R=["Is"], W=["s32"])
    ts(T.I[:, 0:16], s0, 15, None, A.bitwise_and, R=["Is"], W=["Ia"])
    tt(T.tt[:, 0:16], T.s32[:, 0:16], s0, A.mult, R=["s32", "Is"], W=["tt"])
    cp(T.wa[:, 16:32], T.I[:, 0:16], R=["Ia"], W=["wa"])
    tt(T.tt[:, 0:16], T.tt[:, 0:16], T.pre[:, 0:16], A.add, R=["tt", "pre"], W=["tt"])
    mat("LO", 25, 8)
    ts(T.I[:, 64:80], T.tt[:, 0:16], 5, 1023, A.arith_shift_right, A.bitwise_and, R=["tt"], W=["Ic"])
    mat("HE", 9, 9)
    cp(T.cc[:, 0:16], T.I[:, 64:80], R=["Ic"], W=["cc"])
    mat("HO", 17, 9)
    cp(T.Sel[:], T.wdi[:], R=["wdi"], W=["Sel"])
    mat("MW", 17, 10)
    mat("roll", 16, 1.0)
    cp(T.L[:, 65:96:2], s0, R=["Is"], W=["Ls"])
    mat("eye", 0, 1.0)
    mat("neg", 0, -1.0)

    def x_out():
        o = slot(0)
        cp(col(13), T.wti[:], R=["wti"], W=["c13"])
        ts(col(14), col(1), 15.0, None, A.add, R=["c0"], W=["c14"])
        ts(T.m4[:], T.mi[:, 0:128], 112, None, A.bitwise_and, R=["mi"], W=["m4"])
        ts(T.Q8[:], T.mi[:], col(14), SC, A.is_equal, A.mult, R=["mi", "c14"], W=["Q8"])
        ts(col(15), col(6), 16.0, None, A.mult, R=["c0"], W=["c15"])
        cp(T.thb[0:8, :], T.thi[0:8, :], R=["thi"], W=["thb"])
        ts(T.br[0:8, :], T.m4[0:8, :], cF[0:8, 15:16], -1.0, A.is_equal, A.mult, R=["m4", "c15"], W=["br"])
        mm(T.pb6[:, 0:1], T.br[0:8, :], T.thb[0:8, :], True, True, ["br", "thb"], (6,))
        ts(XB[:, o + QW1:o + WTB], T.Q8[:], col(13), 1.0 / SC, A.mult, A.mult, R=["Q8", "c13"], W=["p1"])
        ts(XB[:, o + WTB:o + NTH], T.ones[:, 0:32], col(13), None, A.mult, R=["ones", "c13"], W=["p3"])
        cp(XB[:, o + NTH:o + NTH + 1], T.pb6[:, 0:1], W=["par"], B=(6,))
        ts(XB[:, o:o + 2048], T.xr[:], 128.0, None, A.add, R=["xr", "p1", "p3", "par"], W=["x0"])
        send("x1", ["x0"], "l0")

    def consts():
        ts(T.grp[:], T.m4[:], col(1), -OFF, A.is_equal, A.mult, R=["m4", "c0"], W=["grp"])
        mat("e8", 0, SC)
        mat("e2048", 0, 256.0 * SC)
        mat("roll5", 16, 5.0)
        ts(col(17), col(5), 512.0, None, A.mult, R=["c0"], W=["c17"])
        ts(col(18), col(0), 8.0, None, A.mult, R=["c0"], W=["c18"])
        ts(col(16), col(4), 2.0, col(17), A.mult, A.add, R=["c0", "c17"], W=["c16"])
        ts(T.J[:], T.jj[:], col(0), -1.0 / 256, A.add, A.mult, R=["jj", "c0"], W=["J"])
        ts(T.J1[:], T.jj[:], col(0), 256.0, A.add, A.add, R=["jj", "c0"], W=["J1"])
        ts(T.I8[:], T.jj[:], 8.0, col(18), A.mult, A.add, R=["jj", "c18"], W=["I8"])
        ts(T.POS[:], T.jj[:], 2.0, col(16), A.mult, A.add, R=["jj", "c16"], W=["POS"])
        ts(T.K[:, 1:32:2], T.J[:], -2464.0, 6656.0, A.mult, A.add, R=["J"], W=["K"])
        mat("n2464", 0, -2464.0)
        mat("eye32", 0, 1.0)
        mat("n32", 0, -2464.0 / 256)
        mat("roll32", 16, 1.0 / 256)

    def change(t, hf):
        tt(XB[:, slot(t):slot(t) + XW + 2048].indirect(T.cc[:, 16 + 8 * hf:24 + 8 * hf]), T.oldh[:, 128 * hf:128 * hf + 128], T.zz[:, 128 * hf:128 * hf + 128],
           A.add, R=["oldh", "zz", "cc"], W=["x%d" % t, "x%d" % (t - 1)])

    WZ = ["win1"] + ["wz%d" % j for j in range(5)]
    for t in range(TV):
        end = t == TV - 1
        o, kx = slot(t), "x%d" % t
        x, kg = (XB[:, o:o + 2048], kx) if t else (T.xr[:], "xr")
        up = 128.0 if t else 0.0
        act(T.msk[:], T.EQ[:].indirect(T.wa[:, 16:32]), R=["EQ", "wa"], W=["msk"])
        if t:
            act(T.Sel[:], T.win[:].indirect(T.wa[:, 0:16]), R=["win", "win0", "wa"] + WZ, W=["Sel"])
            mm(T.pb3[:, 0:1], T.one32[:], T.cnt[:], True, True, ["one32", "cnt"], (3,))
            msum(T.pb4[:, 128:144], 4, [(T.roll[:], T.r15[:], ["roll", "r15"]), (T.eye[:], T.J[:], ["eye", "J"]), (T.roll32[:], T.L[:, 1:32:2], ["roll32", "La"])])
            act(T.Fs[:], T.pb3[:, 0:1], W=["Fs"], B=(3,), bias=2048.0)
            act(T.rr[:], T.pb3[:, 0:1], W=["rr"], B=(3,), scale=0.0625, bias=128.46875)
            act(T.r15[:], T.pb4[:, 128:144], AF.Relu, W=["r15"], B=(4,), bias=-1.0)
            act(T.amo[:, t:t + 1], T.rr[:], AF.Identity, R=["rr", "Fs"], W=["amo%d" % t], scale=-16.0, bias=T.Fs[:])
            send("a%d" % t, ["amo%d" % t])
            change(t, 0)
        else:
            mm(T.pb4[:, 128:144], T.roll[:], T.nb[:], True, True, ["roll", "nb"], (4,))
            act(T.r15[:], T.pb4[:, 128:144], AF.Relu, W=["r15"], B=(4,), scale=-1.0, bias=15.0)
        tt(T.R[:], T["tb%d" % t][:].indirect(T.cc[:, 0:16]), T.msk[:], A.mult, R=["tb%d" % t, "cc", "msk"], W=["R"])
        if t:
            change(t, 1)
            send("x%d" % (t + 1) if not end else "xf", [kx], "l%d" % t)
        for half in (1, 0):
            for c in range(4):
                ev, od = slice(c, 256, 8), slice(c + 4, 256, 8)
                out = T["pb5" if c == 0 else "pb6"][:, 64 * c + 32 * half:64 * c + 32 * half + 32]
                E, O = ("HE", "HO") if half else ("LE", "LO")
                msum(out, 5 if c == 0 else 6, [(T[E][:], T.Sel[:, ev], [E, "Sel"]), (T[O][:], T.Sel[:, od], [O, "Sel"])]
                     + ([] if half else [(T.N0[:], T.R[:, ev], ["N0", "R"]), (T.N1[:], T.R[:, od], ["N1", "R"])]))
        cp(T.ll[:, 0:64], T.pb5[:, 0:64], W=["ll0"], B=(5,))
        cp(T.ll[:, 64:256], T.pb6[:, 64:256], W=["ll1"], B=(6,))
        msum(T.pb7[:, 0:256], 7, [(T.MW[:], T.Sel[:], ["MW", "Sel"]), (T.N0[:], T.R[:], ["N0", "R"])])

        def kl(c):
            return "ll0" if c == 0 else "ll1"

        def gather(c, w0=0, w1=64, key=None):
            act(T.G[:, 512 * c + 8 * w0:512 * c + 8 * w1], x.indirect(T.ll[:, 64 * c + w0 // 2:64 * c + w1 // 2]), R=[kg, kl(c)], W=[key or "G%d" % c], bias=OFF - up)

        def d8(c, w0=0, w1=64, key=None, out=None):
            tt(T.d8[:, 512 * c + 8 * w0:512 * c + 8 * w1], x.indirect(T.ll[:, 64 * c + 32 + w0 // 2:64 * c + 32 + w1 // 2]),
               T.G[:, 512 * c + 8 * w0:512 * c + 8 * w1], A.subtract, R=[kg, kl(c), key or "G%d" % c], W=[out or "d8_%d" % c])

        def most(c):
            scan(T.P[:, 512 * c:512 * c + 512], T.RM[:], T.G[:, 512 * c:512 * c + 512], A.mult, A.max, R=["RM", "G%d" % c], W=["P%d" % c])

        def diffs(c):
            for p, (i, j) in enumerate(((0, 1), (0, 3), (1, 4), (2, 5))):
                msum(T["pb%d" % (c % 2)][:, 256 * (c // 2) + p:256 * (c // 2) + 256:4], c % 2,
                     [(T.eye[:], T.G[:, 512 * c + i:512 * c + 512:8], ["eye", "G%d" % c]), (T.neg[:], T.G[:, 512 * c + j:512 * c + 512:8], ["neg", "G%d" % c])])

        def ab13(c):
            act(T.ab13[:, 16 * c:16 * c + 16, :], T["pb%d" % (c % 2)][:, 256 * (c // 2):256 * (c // 2) + 256], AF.Abs, W=["ab13_%d" % c], B=(c % 2,))

        def ab8(c):
            act(T.ab8[:, 16 * c:16 * c + 16, :], T.d8[:, 512 * c:512 * c + 512], AF.Abs, R=["d8_%d" % c], W=["ab8_%d" % c], bias=OFF - up)

        def sum13(c):
            for b in range(4):
                a = c + 4 * b
                mm(T.pb2[:, 1:128:2], T.Q8[:, 15 - a:143 - a], T.ab13[:, 16 * c:16 * c + 16, 4 * b:4 * b + 4], False, a == 15, ["Q8", "ab13_%d" % c], (2,))

        def sum8(c):
            for b in range(4):
                a = c + 4 * b
                mm(T.pb4[:, 0:128], T.Q8[:, 15 - a:143 - a], T.ab8[:, 16 * c:16 * c + 16, 8 * b:8 * b + 8], False, a == 15, ["Q8", "ab8_%d" % c], (4,))

        def sum0(c):
            for b in range(4):
                a = c + 4 * b
                for j, e in ((slice(0, 128, 8), 0), (slice(4, 128, 8), 2), (slice(144, 160), 7)):
                    mm(T.pb2[:, j], XB[:, o + QW1 + 15 - a:o + QW1 + 143 - a], T.P[:, 512 * c + 8 * b + e:512 * c + 512:32], False, False, [kx, "P%d" % c], (2,))

        def limit():
            nth = XB[:, o + NTH:o + NTH + 1]
            if t:
                act(T.Bt[:], T.ones[:, 0:128], AF.Identity, R=["ones", kx, "am%d" % t], W=["Bt"], scale=T.ami[:, t:t + 1], bias=nth)
            else:
                act(T.Bt[:], T.ones[:, 0:128], AF.Identity, R=["ones", kx], W=["Bt"], scale=0.0, bias=nth)

        gather(0, 0, 32, "Ga")
        gather(0, 32, 64)
        if t == 0:
            x_out()
        cp(T.win[:, 0:256], T.pb7[:, 0:256], W=["win0"], B=(7,))
        d8(0, 0, 32, "Ga", "d8_a")
        d8(0, 32, 64)
        dma("Y", "wi%d" % t, [(T.win[0:128 - h, 256 * h:256 * h + 256], T.win[h:128, 0:256]) for h in (1, 3, 8)], R=["win0"] + WZ, W=["win"])
        if t + 2 < TV:
            send("h%d" % (t + 2), ["tb%d" % (t + 1), "win0"])
        if t == 0:
            consts()
        diffs(0)
        mm(T.pb2[:, 0:160], T.eye[:], T.CZ[:], True, False, ["eye", "CZ"], (2,))
        mm(T.pb2[:, 0:160], T.eye[:], T.CY[:], False, False, ["eye", "CY"], (2,))
        mm(T.pb2[:, 0:128:4], T.grp[:], XB[:, o + WTB:o + NTH], False, False, ["grp", kx], (2,))
        mm(T.pb2[:, 144:160], T.grp[:], XB[:, o + WTB:o + WTB + 16], False, False, ["grp", kx], (2,))
        mm(T.pb2[:, 128:144], T.roll5[:], T.L[:, 65:96:2], False, False, ["roll5", "Ls"], (2,))
        for j in (2, 6):
            mm(T.pb2[:, j:128:8], T.e8[:], T.r15[:], False, False, ["e8", "r15"], (2,))
        if not end:
            mm(T.pb5[:, 64:96], T.eye32[:], T.K[:], True, False, ["eye32", "K"], (5,))
            for j in (0, 1):
                mm(T.pb5[:, 64 + j:96:2], T.n2464[:], T.r15[:], False, False, ["n2464", "r15"], (5,))
        most(0)
        gather(1)
        diffs(1)
        sum0(0)
        d8(1)
        most(1)
        gather(2)
        ab13(0)
        diffs(2)
        sum0(1)
        sum13(0)
        most(2)
        d8(2)
        gather(3)
        most(3)
        ab13(1)
        sum0(2)
        diffs(3)
        sum13(1)
        sum0(3)
        limit()
        ab13(2)
        sum13(2)
        mm(T.pb2[:, 1:128:2], T.e8[:], T.Bt[:, 0:64], False, False, ["e8", "Bt"], (2,))
        ab13(3)
        sum13(3)
        mm(T.pb4[:, 0:128], T.e8[:], T.Bt[:], True, False, ["e8", "Bt"], (4,))
        mm(T.pb4[:, 0:128:8], T.e2048[:], T.r15[:], False, False, ["e2048", "r15"], (4,))
        d8(3, 0, 32, None, "d8_b")
        ab8(0)
        sum8(0)
        n = t + 1
        scan(T.MZ[:], T.Z0[:], T.pb2[:, 0:128], A.min, A.max, R=["Z0"], W=["MZ"], B=(2,))
        tt(T.M13[:], T.MZ[:, 2:128:8], T.MZ[:, 7:128:8], A.min, R=["MZ"], W=["M13"])
        tt(T.pre[:, 0:32:2], T.pb2[:, 128:144], T.MZ[:, 0:128:8], A.add, R=["MZ"], W=["pre0"], B=(2,))
        tt(T.pre[:, 1:32:2], T.pb2[:, 144:160], T.M13[:], A.min, R=["M13"], W=["pre"], B=(2,))
        d8(3, 32, 64)
        ts(T.hw[:], T.pre[:, 1:32:2], TAG - 8, 7 * 256, A.arith_shift_right, A.bitwise_and, R=["pre"], W=["hw"])
        ts(T.hm[:], T.pre[:, 1:32:2], TAG, None, A.arith_shift_right, R=["pre"], W=["hm"])
        ts(T.I[:, 32:64], T.pre[:], 4095, None, A.bitwise_and, R=["pre", "pre0"], W=["Is"])
        tt(T.DX[:, 1:32:2], T.hw[:], T.J1[:], A.add, R=["hw", "J1"], W=["Dh"])
        ts(T.s7[:], T.pre[:, 1:32:2], 7, None, A.bitwise_and, R=["pre"], W=["s7"])
        tt(T.zF[:], T.hm[:], T.POS[:], A.add, R=["hm", "POS"], W=["zF"])
        if not end:
            mm(T.pb5[:, 65:96:2], T.n32[:], T.DX[:, 1:32:2], False, True, ["n32", "Dh"], (5,))
            ts(T.s32[:], T.I[:, 32:64], 32.0, None, A.add, R=["Is"], W=["s32"])
        tt(T.DX[:, 129:160:2], T.s7[:], T.I8[:], A.add, R=["s7", "I8"], W=["Dc"])
        cp(T.zl[:], T.zF[:], R=["zF"], W=["zl"])
        if not end:
            tt(T.tt[:], T.s32[:], T.I[:, 32:64], A.mult, R=["s32", "Is"], W=["tt"])
        cp(T.ol[:], T.DX[:, 129:160:2], R=["Dc"], W=["ol"])
        ts(T.f13[:], T.hm[:], 7.0, None, A.is_ge, R=["hm"], W=["f13"])
        if not end:
            tt(T.tt[:], T.pb5[:, 64:96], T.tt[:], A.add, R=["tt"], W=["tt"], B=(5,))
            ts(T.I[:, 0:32], T.pre[:], 15, None, A.bitwise_and, R=["pre"], W=["Ia"])
            ts(T.I[:, 64:96], T.tt[:], 5, 1023, A.arith_shift_right, A.bitwise_and, R=["tt"], W=["Ic"])
        tt(T.DX[:, 32:128:2], T.I[:, 0:96:2], T.I[:, 1:96:2], A.subtract, R=["Is", "Ia", "Ic"], W=["Dd"])
        cp(T.DX[:, 33:128:2], T.I[:, 1:96:2], R=["Is", "Ia", "Ic"], W=["Dx"])
        if end:
            ts(T.zz[:], T.P[:].indirect(T.zl[:]), 0.5, None, A.mult, R=["P0", "P1", "P2", "P3", "zl"], W=["zz"])
            send("of", ["ol"])
            send("zf", ["zz"])
        for c in (1, 2, 3):
            ab8(c)
            sum8(c)
        if not end:
            act(T.zz[:], T.P[:].indirect(T.zl[:]), R=["P0", "P1", "P2", "P3", "zl"], W=["zz"], scale=0.5)
            act(T.oldh[:], XB[:, slot(n):slot(n) + 2048].indirect(T.ol[:]), R=["x%d" % n, "ol"], W=["oldh"], scale=0.5, bias=56.0)
        scan(T.M8[:], T.RM[:, 0:128], T.pb4[:, 0:128], A.mult, A.max, R=["RM"], W=["M8"], B=(4,))
        for j in (0, 1):
            tt(T.F[:, 32 * j + 1:32 * j + 32:2], T.M8[:, 7:128:8], T.f13[:], A.min, R=["M8", "f13", "F"], W=["F%d" % j])
        pairs = [(0, "La", "wa", ["Dh", "dw"]), (96, "Lc", "cc", ["Dc", "dc"])]
        for c0, k, _, more in pairs[::-1] if end else pairs:
            scan(T.L[:, c0:c0 + 64], T.F[:], T.DX[:, c0:c0 + 64], A.mult, A.add, R=["F0", "F1", "Dd", "Dx"] + more, W=[k])
        for c0, k, out, _ in pairs[::-1] if end else pairs:
            cp(T[out][:], T.L[:, c0 + 1:c0 + 64:2], R=[k], W=[out])
        scan(T.L[:, 64:96], T.F[:, 0:32], T.DX[:, 64:96], A.mult, A.add, R=["F0", "Dd", "Dx"], W=["Ls"])
        if not end:
            act(T.junk[:], T.F[:, 1:32:2], R=["F0"], W=["junk", "cnt"], accum_out=T.cnt[:])

    send("cf", ["cc"])
    act(T.hs[:], T.win[:].indirect(T.wa[:, 0:16]), R=["win", "win0", "wa"] + WZ, W=["hs"])
    ts(T.IND[:], T.mi[:, 0:32], col(0), None, A.is_gt, R=["mi", "c0"], W=["IND"])
    ts(T.zF[:], T.L[:, 1:32:2], -1.0 / 256, 16.0, A.mult, A.add, R=["La"], W=["zF"])
    tt(T.M13[:], T.r15[:], T.J[:], A.add, R=["r15", "J"], W=["M13"])
    cp(T.nst[:, 16:32], T.L[:, 65:96:2], R=["Ls"], W=["nst2"])
    tt(T.nst[:, 0:16], T.zF[:], T.M13[:], A.subtract, R=["zF", "M13"], W=["nst"])
    cp(T.zl[:], T.nst[:, 0:16], R=["nst"], W=["zl"])
    run("V", lambda: g.vector.transpose(T.nsx[:], T.nst[:]), ["nst", "nst2"], ["nsx"])
    tt(T.yws[:], T.IND[:].indirect(T.zl[:]), T.hs[:], A.mult, R=["IND", "zl", "hs"], W=["yws"])
    send("yf", ["yws"])
    send("nf", ["nsx"])
    ts(T.oldh[:], XB[:, 0:2048].indirect(T.of[:]), 0.5, 56.0, A.mult, A.add, R=["x%d" % TV, "of"], W=["oldh"])
    tt(XB[:, 0:XW + 2048].indirect(T.cf[:]), T.oldh[:], T.zf[:], A.add, R=["oldh", "zf", "cf"], W=["x%d" % TV, "x%d" % (TV - 1), "xp"])
    ts(T.xo[:, 0:1408], XB[:, 0:1408], -128.0, None, A.add, R=["x%d" % TV], W=["xo0"])
    act(T.xo[:, 1408:2048], XB[:, 1408:2048], R=["x%d" % TV], W=["xo1"], bias=-128.0)
    ys = []
    for a in range(4):
        for b in range(2):
            for k, y in enumerate((T.yn, T.ys)):
                ys.append((y[2 * a + b:2 * a + b + 1, :], T.nsr[32 * a + 16 * k:32 * a + 16 * k + 16, 16 * b:16 * b + 16]))
    dma("Y", "o_w", [(T.yw[:], T.ywr[:])], R=["ywr"])
    dma("Y", "o_ns", ys, R=["nsr"])
    dma("Y", "o_x0", [(T.yx[:, 0:1408], T.xo[:, 0:1408])], R=["xo0"])
    dma("S", "o_x1", [(T.yx[:, 1408:2048], T.xo[:, 1408:2048])], R=["xo1"])
    for s in total:
        need("G" if s == "L" else "Y", (s, total[s]))
